import numpy as np
import ml_dtypes


def mxq(x, axis, fmt="e4m3"):
    dtype, down = {"e4m3": (ml_dtypes.float8_e4m3fn, 7), "e5m2": (ml_dtypes.float8_e5m2, 14)}[fmt]
    v = np.moveaxis(np.asarray(x, np.float32).astype(ml_dtypes.bfloat16).astype(np.float64), axis, -1)
    blocks = v.reshape(v.shape[:-1] + (-1, 32))
    amax = np.abs(blocks).max(-1, keepdims=True)
    byte = np.maximum(np.where(amax > 0, np.frexp(amax)[1] - 1 + 127, 0) - down, 1)
    scale = np.exp2(byte - 127.0)
    codes = (blocks / scale).astype(np.float32).astype(dtype).astype(np.float64)
    return np.moveaxis((codes * scale).reshape(v.shape), -1, axis)


WIDE = False


def mx_kscale(k):
    if not WIDE:
        return np.ones(k)
    levels = np.array([10, -10, 5, -5, 0])
    if k % 512:
        return np.exp2(np.random.permutation(np.resize(levels, k // 32))).repeat(32)
    a = np.empty((k // 512, 16))
    for p in range(k // 512):
        a[p, :8] = np.random.permutation(np.resize(levels, 8))
        for g in range(8):
            far = levels[np.abs(levels - a[p, g]) >= 10]
            a[p, g + 8] = far[np.random.randint(len(far))]
    return np.exp2(a.ravel()).repeat(32)


def f64(x):
    return np.asarray(x).astype(np.float64)


def striped(idx):
    return np.tile(idx.reshape(-1, 16).T, (8, 1)).astype(np.uint16)


def unstriped(offs):
    return offs[:16].T.reshape(-1).astype(np.int64)


def striped8(idx):
    return np.concatenate([x.reshape(-1, 16).T for x in idx]).astype(np.uint16)


def runs(offs, k):
    lists = np.stack([offs[16 * r : 16 * r + 16].T.reshape(-1) for r in range(8)]).astype(np.int64)
    return lists[np.arange(k) % 512 // 64]


def pack_weight(w):
    k, n = w.shape
    w = f64(np.asarray(w, np.float32).astype(ml_dtypes.bfloat16)).reshape(k // 32, 32, n)
    amax = np.abs(w).max(1)
    byte = np.clip(np.where(amax > 0, np.frexp(amax)[1] - 1 + 127 - 7, 1), 1, 254)
    scaled = (w * np.exp2(127.0 - byte)[:, None, :]).reshape(k, n).astype(np.float32)
    words = np.ascontiguousarray(scaled.reshape(k // 512, 128, 4, n).transpose(0, 1, 3, 2)).astype(ml_dtypes.float8_e4m3fn).view(np.uint8)
    return words, np.ascontiguousarray(byte.astype(np.uint8).reshape(k // 512, 16, n))


def unpack_weight(words, scales):
    g, p, n, _ = words.shape
    vals = np.ascontiguousarray(words).view(ml_dtypes.float8_e4m3fn).astype(np.float64) * np.repeat(np.exp2(scales.astype(np.float64) - 127.0), 8, axis=1)[..., None]
    return vals.transpose(0, 1, 3, 2).reshape(g * 512, n)


E2M1 = np.array([0.0, 0.5, 1.0, 1.5, 2.0, 3.0, 4.0, 6.0, -0.0, -0.5, -1.0, -1.5, -2.0, -3.0, -4.0, -6.0])


def pack_fp4(w):
    k, n = w.shape
    w = f64(np.asarray(w, np.float32).astype(ml_dtypes.bfloat16)).reshape(k // 32, 32, n)
    amax = np.abs(w).max(1)
    mant, ex = np.frexp(amax / 6.0)
    byte = np.clip(np.where(amax > 0, np.where(mant > 0.5, ex, ex - 1) + 127, 1), 1, 254)
    scaled = (w * np.exp2(127.0 - byte)[:, None, :]).reshape(k, n).astype(np.float32)
    c = np.ascontiguousarray(scaled.reshape(k // 512, 128, 4, n).transpose(0, 1, 3, 2)).astype(ml_dtypes.float4_e2m1fn).view(np.uint8) & 0xF
    words = (c[..., 0::2] | (c[..., 1::2] << 4)).reshape(k // 512, 128, 2 * n)
    return np.ascontiguousarray(words), np.ascontiguousarray(byte.astype(np.uint8).reshape(k // 512, 16, n))


def unpack_fp4(words, scales):
    g, _, n = scales.shape
    words = np.ascontiguousarray(words).reshape(g, 128, n, 2)
    nib = np.empty((g, 128, n, 4), np.uint8)
    nib[..., 0::2] = words & 0xF
    nib[..., 1::2] = words >> 4
    vals = E2M1[nib] * np.repeat(np.exp2(scales.astype(np.float64) - 127.0), 8, axis=1)[..., None]
    return vals.transpose(0, 1, 3, 2).reshape(g * 512, n)


def planes(y):
    n, m = y.shape
    v = y.astype(np.float32).astype(ml_dtypes.bfloat16).astype(np.float64).reshape(n // 32, 32, m)
    top = np.abs(v).max(1)
    byte = np.clip(np.where(top > 0, np.frexp(top)[1] - 1 + 127 - 7, 1), 1, 254)
    codes = (v * np.exp2(127.0 - byte)[:, None, :]).reshape(n, m).astype(np.float32).astype(ml_dtypes.float8_e4m3fn).view(np.uint8)
    words = codes.reshape(n // 512, 128, 4, m).transpose(0, 1, 3, 2)
    return np.ascontiguousarray(words), np.ascontiguousarray(byte.astype(np.uint8).reshape(n // 512, 16, m))


K, T, S, N, H = 512, 2048, 512, 512, 512


def setup_inputs():
    n = np.random.standard_normal
    s = mx_kscale(K)[:, None]
    u = mx_kscale(S)
    packed_xT = pack_weight(n((K, T)) * s)
    packed_w1 = pack_fp4(n((S, N)) / np.sqrt(S) / u[:, None])
    return {
        "x_words": packed_xT[0],
        "x_scales": packed_xT[1],
        "wa": (n((K, H)) / np.sqrt(K) / s).astype(np.float32),
        "wb": (n((K, H)) / np.sqrt(K) / s).astype(np.float32),
        "gt": (np.random.uniform(0.5, 1.5, (S, 1)) * u[:, None]).astype(np.float32),
        "w1_words": packed_w1[0],
        "w1_scales": packed_w1[1],
        "offs": striped(np.random.permutation(T)[:S]),
        "two": striped(np.random.permutation(T)[:S]),
        "fl": striped8(np.stack([np.random.permutation(H) for _ in range(8)])),
    }


def reference(x_words, x_scales, wa, wb, gt, w1_words, w1_scales, offs, two, fl):
    xq = unpack_weight(x_words, x_scales)[:, unstriped(offs)]
    a = xq.T @ mxq(f64(wa), 0, "e4m3")
    x_two = unpack_weight(x_words, x_scales)[:, unstriped(two)]
    b = x_two.T @ mxq(f64(wb), 0, "e4m3")
    bq = b[np.arange(S)[:, None], runs(fl, S)]
    z = f64(gt) * np.maximum(a, bq)
    out_0 = unpack_fp4(w1_words, w1_scales).T @ mxq(z, 0, "e4m3")
    return (out_0,) + planes(out_0)

@@ -1,0 +1,256 @@
+from contextlib import ExitStack
+
+import concourse.mybir as mybir
+
+K, T, S, N, H = 512, 2048, 512, 512, 512
+FLOPS = 2 * S * K * H * 2 + 2 * S * N * H
+
+F32 = mybir.dt.float32
+BF16 = mybir.dt.bfloat16
+I32 = mybir.dt.int32
+U32 = mybir.dt.uint32
+U16 = mybir.dt.uint16
+U8 = mybir.dt.uint8
+FP8X4 = mybir.dt.float8_e4m3fn_x4
+FP4X4 = mybir.dt.float4_e2m1fn_x4
+ACT = mybir.ActivationFunctionType
+ALU = mybir.AluOpType
+
+P = 128
+PACK = 4
+HALF = H // 2
+CHUNK = 128
+CHUNKS = H // CHUNK
+LINE = 4
+
+
+def tile_picked_tokmax_none_po_kernel(
+    tc, x_words, x_scales, wa, wb, gt, w1_words, w1_scales, offs, two, fl, out_0, out_1, out_2
+):
+    nc = tc.nc
+    with ExitStack() as ctx:
+        keep = ctx.enter_context(tc.tile_pool(name="keep", bufs=1))
+        psum = ctx.enter_context(tc.psum_pool(name="psum", bufs=1))
+
+        def sb(shape, dtype, name):
+            return keep.tile(shape, dtype, name=name, align_bytes=64)
+
+        def bank(i, shape, name):
+            return psum.tile(shape, F32, name=name, tag="bank%d" % i)
+
+        offs_t = keep.tile([P, S // 16], U16, name="offs_t")
+        two_t = keep.tile([P, S // 16], U16, name="two_t")
+        fl_t = keep.tile([P, H // 16], U16, name="fl_t")
+        xw = sb([P, T], I32, "xw")
+        xs = sb([P, T], U8, "xs")
+        w1w = sb([P, 2 * N], U8, "w1w")
+        w1s = sb([P, N], U8, "w1s")
+        g = sb([P, PACK], F32, "g")
+        wb_raw = [sb([P, PACK, HALF], F32, "wb_raw%d" % h) for h in range(2)]
+        wa_raw = [sb([P, PACK, HALF], F32, "wa_raw%d" % h) for h in range(2)]
+
+        nc.vector.memset(xs[:].bitcast(I32), 0)
+        nc.vector.memset(w1s[:].bitcast(I32), 0)
+
+        wb_v = wb.rearrange("(p j) c -> p j c", j=PACK)
+        wa_v = wa.rearrange("(p j) c -> p j c", j=PACK)
+        nc.sync.dma_start(two_t[:], two)
+        nc.sync.dma_start(offs_t[:], offs)
+        nc.sync.dma_start(out=wb_raw[0][:], in_=wb_v[:, :, 0:HALF])
+        for q in range(4):
+            nc.sync.dma_start(out=xs[32 * q : 32 * q + 4, :].bitcast(I32), in_=x_scales[0, 4 * q : 4 * q + 4, :].bitcast(I32))
+        nc.sync.dma_start(out=wb_raw[1][:], in_=wb_v[:, :, HALF:H])
+        nc.sync.dma_start(out=w1w[:].bitcast(I32), in_=w1_words[0].bitcast(I32))
+        nc.sync.dma_start(out=xw[:], in_=x_words[0].rearrange("p n t -> p (n t)").bitcast(I32))
+        nc.sync.dma_start(out=g[:], in_=gt.rearrange("(p t) o -> p (t o)", t=PACK))
+        nc.sync.dma_start(fl_t[:], fl)
+        for h in range(2):
+            nc.sync.dma_start(out=wa_raw[h][:], in_=wa_v[:, :, h * HALF : (h + 1) * HALF])
+        for q in range(4):
+            nc.sync.dma_start(out=w1s[32 * q : 32 * q + 4, :].bitcast(I32), in_=w1_scales[0, 4 * q : 4 * q + 4, :].bitcast(I32))
+
+        def cast_half(raw, grouped):
+            nc.scalar.copy(
+                out=grouped.rearrange("p (c i j) -> p c j i", i=LINE, j=PACK),
+                in_=raw[:].rearrange("p j (c i) -> p c j i", i=LINE),
+            )
+
+        def quantize(codes, scales, values):
+            nc.vector.quantize_mx(out=codes.bitcast(FP8X4), scales=scales, in_=values)
+
+        def gather_scales(lst, name):
+            plain = sb([P, S], U8, name + "_plain")
+            nc.vector.tensor_copy(plain[:], xs[:].indirect(lst[:]))
+            return plain
+
+        def deal_bytes(plain, name):
+            dealt = sb([P, S], U8, name)
+            nc.vector.tensor_copy(
+                out=dealt[:].rearrange("p (t m) -> p t m", t=PACK),
+                in_=plain[:].rearrange("p (m t) -> p t m", t=PACK),
+            )
+            return dealt
+
+        def gather_words(lst, name):
+            dealt = sb([P, S], U32, name)
+            nc.vector.tensor_copy(dealt[:].rearrange("p (t m) -> p m t", t=PACK), xw[:].bitcast(U32).indirect(lst[:]))
+            return dealt
+
+        sb_plain = gather_scales(two_t, "xb_s")
+        sa_plain = gather_scales(offs_t, "xa_s")
+        xb_s = deal_bytes(sb_plain, "xb_s")
+        xa_s = deal_bytes(sa_plain, "xa_s")
+
+        wb_g = [sb([P, HALF * PACK], BF16, "wb_g%d" % h) for h in range(2)]
+        wa_g = [sb([P, HALF * PACK], BF16, "wa_g%d" % h) for h in range(2)]
+        wb_c = sb([P, H], U32, "wb_c")
+        wb_s = sb([P, H], U8, "wb_s")
+        wa_c = [sb([P, HALF], U32, "wa_c%d" % h) for h in range(2)]
+        wa_s = [sb([P, HALF], U8, "wa_s%d" % h) for h in range(2)]
+
+        g_abs = sb([P, PACK], F32, "g_abs")
+        g_sign = sb([P, CHUNK, PACK], BF16, "g_sign")
+        for h in range(2):
+            cast_half(wb_raw[h], wb_g[h][:])
+        nc.scalar.activation(out=g_abs[:], in_=g[:], func=ACT.Abs)
+        nc.scalar.activation(out=g_sign[:], in_=g[:].unsqueeze(1).to_broadcast([P, CHUNK, PACK]), func=ACT.Sign)
+
+        w1w_d = sb([P, 2 * N], U8, "w1w_d")
+        nc.vector.tensor_copy(
+            out=w1w_d[:].rearrange("p (t m b) -> p t m b", t=PACK, b=2),
+            in_=w1w[:].rearrange("p (m t b) -> p t m b", t=PACK, b=2),
+        )
+
+        for h in range(2):
+            quantize(wb_c[:, h * HALF : (h + 1) * HALF], wb_s[:, h * HALF : (h + 1) * HALF], wb_g[h][:])
+
+        xb_w = gather_words(two_t, "xb_w")
+        xa_w = gather_words(offs_t, "xa_w")
+
+        def rows(t):
+            return slice(t * P, (t + 1) * P)
+
+        cast_half(wa_raw[0], wa_g[0][:])
+        quantize(wa_c[0][:], wa_s[0][:], wa_g[0][:])
+
+        b_sb = []
+        for t in range(PACK):
+            acc = bank(t, [P, H], "b_acc%d" % t)
+            nc.tensor.matmul_mx(
+                out=acc[:], lhsT=xb_w[:, rows(t)].bitcast(FP8X4), lhsT_scale=xb_s[:, rows(t)],
+                rhs=wb_c[:].bitcast(FP8X4), rhs_scale=wb_s[:], start=True, stop=True,
+            )
+            b_t = sb([P, H], F32, "b_sb%d" % t)
+            nc.scalar.activation(out=b_t[:], in_=acc[:], func=ACT.Copy, scale=g_abs[:, t : t + 1])
+            b_sb.append(b_t)
+
+        def project_a(h):
+            a_h = sb([P, PACK, HALF], F32, "a_sb%d" % h)
+            for u in range(2):
+                acc = bank(4 + 2 * h + u, [P, 2, HALF], "a_acc%d_%d" % (h, u))
+                for v in range(2):
+                    t = 2 * u + v
+                    nc.tensor.matmul_mx(
+                        out=acc[:, v, :], lhsT=xa_w[:, rows(t)].bitcast(FP8X4), lhsT_scale=xa_s[:, rows(t)],
+                        rhs=wa_c[h][:].bitcast(FP8X4), rhs_scale=wa_s[h][:], start=True, stop=True,
+                    )
+                for v in range(2):
+                    t = 2 * u + v
+                    nc.scalar.activation(out=a_h[:, t, :], in_=acc[:, v, :], func=ACT.Copy, scale=g_abs[:, t : t + 1])
+            return a_h
+
+        def gather_b(c0, width, name):
+            bq = sb([P, PACK, width], F32, name)
+            for t in range(PACK):
+                nc.vector.tensor_copy(bq[:, t, :], b_sb[t][:].indirect(fl_t[:, c0 // 16 : (c0 + width) // 16]))
+            return bq
+
+        def walk(ap):
+            return ap.rearrange("p t (c i) -> p c t i", i=LINE)
+
+        def larger(c, a_ap, bq_ap):
+            zu = sb([P, CHUNK * PACK], BF16, "zu%d" % c)
+            nc.vector.tensor_tensor(
+                out=zu[:].rearrange("p (c i t) -> p c t i", i=LINE, t=PACK), in0=walk(a_ap), in1=walk(bq_ap), op=ALU.max
+            )
+            return zu
+
+        def signed(c, zu):
+            z = sb([P, CHUNK * PACK], BF16, "z%d" % c)
+            nc.vector.tensor_tensor(out=z[:], in0=zu[:], in1=g_sign[:].rearrange("p n t -> p (n t)"), op=ALU.mult)
+            return z
+
+        def quantize_z(c, z):
+            z_c = sb([P, CHUNK], U32, "z_c%d" % c)
+            z_s = sb([P, CHUNK], U8, "z_s%d" % c)
+            quantize(z_c[:], z_s[:], z[:])
+            return z_c, z_s
+
+        def mix(acc_ap, t, z_c, z_s):
+            nc.tensor.matmul_mx(
+                out=acc_ap, lhsT=w1w_d[:, 2 * P * t : 2 * P * (t + 1)].bitcast(FP4X4), lhsT_scale=w1s_d[:, rows(t)],
+                rhs=z_c[:].bitcast(FP8X4), rhs_scale=z_s[:], start=True, stop=True,
+            )
+
+        out_v = out_0.rearrange("(p t) j -> p t j", t=PACK)
+        words_v = out_1[0].rearrange("p n r -> p (n r)").bitcast(I32)
+        y_s = sb([P, H], U8, "y_s")
+
+        def mix_chunk(c, z_c, z_s):
+            cols = slice(c * CHUNK, (c + 1) * CHUNK)
+            y = sb([P, PACK, CHUNK], F32, "y%d" % c)
+            yg = sb([P, CHUNK * PACK], BF16, "yg%d" % c)
+            if c < CHUNKS - 1:
+                acc = bank(c, [P, PACK, CHUNK], "y_acc%d" % c)
+                for t in range(PACK):
+                    mix(acc[:, t, :], t, z_c, z_s)
+                nc.scalar.copy(out=y[:], in_=acc[:])
+                nc.sync.dma_start(out=out_v[:, :, cols], in_=y[:])
+                nc.scalar.copy(out=yg[:].rearrange("p (n t) -> p n t", t=PACK), in_=acc[:].rearrange("p t n -> p n t"))
+            else:
+                accs = [bank(3 + u, [P, 2, CHUNK], "y_acc%d_%d" % (c, u)) for u in range(2)]
+                for t in range(PACK):
+                    mix(accs[t // 2][:, t % 2, :], t, z_c, z_s)
+                nc.scalar.copy(out=y[:, 0:2, :], in_=accs[0][:])
+                nc.vector.tensor_copy(out=y[:, 2:4, :], in_=accs[1][:])
+                nc.sync.dma_start(out=out_v[:, :, cols], in_=y[:])
+                nc.vector.tensor_copy(out=yg[:].rearrange("p (c i t) -> p c t i", i=LINE, t=PACK), in_=walk(y[:]))
+            return yg
+
+        def planes(c, yg):
+            cols = slice(c * CHUNK, (c + 1) * CHUNK)
+            y_c = sb([P, CHUNK], I32, "y_c%d" % c)
+            quantize(y_c[:], y_s[:, cols], yg[:])
+            nc.sync.dma_start(out=words_v[:, cols], in_=y_c[:])
+
+        a0 = project_a(0)
+        cast_half(wa_raw[1], wa_g[1][:])
+        bq01 = gather_b(0, HALF, "bq01")
+        w1s_d = deal_bytes(w1s, "w1s_d")
+        quantize(wa_c[1][:], wa_s[1][:], wa_g[1][:])
+        a1 = project_a(1)
+        bq2 = gather_b(2 * CHUNK, CHUNK, "bq2")
+        zu0 = larger(0, a0[:, :, 0:CHUNK], bq01[:, :, 0:CHUNK])
+        zu1 = larger(1, a0[:, :, CHUNK:HALF], bq01[:, :, CHUNK:HALF])
+        z0 = signed(0, zu0)
+        z1 = signed(1, zu1)
+        q0 = quantize_z(0, z0)
+        q1 = quantize_z(1, z1)
+        yg0 = mix_chunk(0, *q0)
+        yg1 = mix_chunk(1, *q1)
+        zu2 = larger(2, a1[:, :, 0:CHUNK], bq2[:])
+        bq3 = gather_b(3 * CHUNK, CHUNK, "bq3")
+        z2 = signed(2, zu2)
+        zu3 = larger(3, a1[:, :, CHUNK:HALF], bq3[:])
+        q2 = quantize_z(2, z2)
+        z3 = signed(3, zu3)
+        yg2 = mix_chunk(2, *q2)
+        planes(0, yg0)
+        q3 = quantize_z(3, z3)
+        planes(1, yg1)
+        yg3 = mix_chunk(3, *q3)
+        planes(2, yg2)
+        planes(3, yg3)
+        for q in range(4):
+            eng = nc.scalar if q % 2 else nc.sync
+            eng.dma_start(out=out_2[0, 4 * q : 4 * q + 4, :].bitcast(I32), in_=y_s[32 * q : 32 * q + 4, :].bitcast(I32))

@@ -54,20 +54,22 @@ def tile_picked_tokmax_none_po_kernel(
 
         wb_v = wb.rearrange("(p j) c -> p j c", j=PACK)
         wa_v = wa.rearrange("(p j) c -> p j c", j=PACK)
-        nc.sync.dma_start(two_t[:], two)
-        nc.sync.dma_start(offs_t[:], offs)
-        nc.sync.dma_start(out=wb_raw[0][:], in_=wb_v[:, :, 0:HALF])
-        for q in range(4):
-            nc.sync.dma_start(out=xs[32 * q : 32 * q + 4, :].bitcast(I32), in_=x_scales[0, 4 * q : 4 * q + 4, :].bitcast(I32))
-        nc.sync.dma_start(out=wb_raw[1][:], in_=wb_v[:, :, HALF:H])
+        def load_scale_rows(dst, src):
+            for q in range(4):
+                nc.sync.dma_start(out=dst[32 * q : 32 * q + 4, :].bitcast(I32), in_=src[0, 4 * q : 4 * q + 4, :].bitcast(I32))
+
         nc.sync.dma_start(out=w1w[:].bitcast(I32), in_=w1_words[0].bitcast(I32))
+        nc.sync.dma_start(two_t[:], two)
+        nc.sync.dma_start(out=wb_raw[0][:], in_=wb_v[:, :, 0:HALF])
+        load_scale_rows(xs, x_scales)
+        nc.sync.dma_start(out=wb_raw[1][:], in_=wb_v[:, :, HALF:H])
+        nc.sync.dma_start(offs_t[:], offs)
         nc.sync.dma_start(out=xw[:], in_=x_words[0].rearrange("p n t -> p (n t)").bitcast(I32))
+        nc.sync.dma_start(out=wa_raw[0][:], in_=wa_v[:, :, 0:HALF])
         nc.sync.dma_start(out=g[:], in_=gt.rearrange("(p t) o -> p (t o)", t=PACK))
         nc.sync.dma_start(fl_t[:], fl)
-        for h in range(2):
-            nc.sync.dma_start(out=wa_raw[h][:], in_=wa_v[:, :, h * HALF : (h + 1) * HALF])
-        for q in range(4):
-            nc.sync.dma_start(out=w1s[32 * q : 32 * q + 4, :].bitcast(I32), in_=w1_scales[0, 4 * q : 4 * q + 4, :].bitcast(I32))
+        nc.sync.dma_start(out=wa_raw[1][:], in_=wa_v[:, :, HALF:H])
+        load_scale_rows(w1s, w1_scales)
 
         def cast_half(raw, grouped):
             nc.scalar.copy(
@@ -96,34 +98,29 @@ def tile_picked_tokmax_none_po_kernel(
             nc.vector.tensor_copy(dealt[:].rearrange("p (t m) -> p m t", t=PACK), xw[:].bitcast(U32).indirect(lst[:]))
             return dealt
 
-        sb_plain = gather_scales(two_t, "xb_s")
-        sa_plain = gather_scales(offs_t, "xa_s")
-        xb_s = deal_bytes(sb_plain, "xb_s")
-        xa_s = deal_bytes(sa_plain, "xa_s")
-
-        wb_g = [sb([P, HALF * PACK], BF16, "wb_g%d" % h) for h in range(2)]
-        wa_g = [sb([P, HALF * PACK], BF16, "wa_g%d" % h) for h in range(2)]
-        wb_c = sb([P, H], U32, "wb_c")
-        wb_s = sb([P, H], U8, "wb_s")
-        wa_c = [sb([P, HALF], U32, "wa_c%d" % h) for h in range(2)]
-        wa_s = [sb([P, HALF], U8, "wa_s%d" % h) for h in range(2)]
-
-        g_abs = sb([P, PACK], F32, "g_abs")
-        g_sign = sb([P, CHUNK, PACK], BF16, "g_sign")
-        for h in range(2):
-            cast_half(wb_raw[h], wb_g[h][:])
-        nc.scalar.activation(out=g_abs[:], in_=g[:], func=ACT.Abs)
-        nc.scalar.activation(out=g_sign[:], in_=g[:].unsqueeze(1).to_broadcast([P, CHUNK, PACK]), func=ACT.Sign)
-
         w1w_d = sb([P, 2 * N], U8, "w1w_d")
         nc.vector.tensor_copy(
             out=w1w_d[:].rearrange("p (t m b) -> p t m b", t=PACK, b=2),
             in_=w1w[:].rearrange("p (m t b) -> p t m b", t=PACK, b=2),
         )
+        sb_plain = gather_scales(two_t, "xb_s")
+        sa_plain = gather_scales(offs_t, "xa_s")
+        xb_s = deal_bytes(sb_plain, "xb_s")
+        xa_s = deal_bytes(sa_plain, "xa_s")
+
+        wb_g = sb([P, H * PACK], BF16, "wb_g")
+        wa_g = [
+            sb([P, HALF * PACK], BF16, "wa_g0"),
+            keep.tile([P, HALF * PACK], BF16, name="wa_g1", tag="late", align_bytes=64),
+        ]
+        wb_c = sb([P, H], U32, "wb_c")
+        wb_s = sb([P, H], U8, "wb_s")
+        wa_c = [sb([P, HALF], U32, "wa_c%d" % h) for h in range(2)]
+        wa_s = [sb([P, HALF], U8, "wa_s%d" % h) for h in range(2)]
 
         for h in range(2):
-            quantize(wb_c[:, h * HALF : (h + 1) * HALF], wb_s[:, h * HALF : (h + 1) * HALF], wb_g[h][:])
-
+            cast_half(wb_raw[h], wb_g[:, h * HALF * PACK : (h + 1) * HALF * PACK])
+        quantize(wb_c[:], wb_s[:], wb_g[:])
         xb_w = gather_words(two_t, "xb_w")
         xa_w = gather_words(offs_t, "xa_w")
 
@@ -132,6 +129,11 @@ def tile_picked_tokmax_none_po_kernel(
 
         cast_half(wa_raw[0], wa_g[0][:])
         quantize(wa_c[0][:], wa_s[0][:], wa_g[0][:])
+
+        g_abs = sb([P, PACK], F32, "g_abs")
+        g_sign = sb([P, PACK], BF16, "g_sign")
+        nc.scalar.activation(out=g_abs[:], in_=g[:], func=ACT.Abs)
+        nc.scalar.activation(out=g_sign[:], in_=g[:], func=ACT.Sign)
 
         b_sb = []
         for t in range(PACK):
@@ -145,7 +147,7 @@ def tile_picked_tokmax_none_po_kernel(
             b_sb.append(b_t)
 
         def project_a(h):
-            a_h = sb([P, PACK, HALF], F32, "a_sb%d" % h)
+            a_h = sb([P, PACK, HALF], BF16, "a_sb%d" % h)
             for u in range(2):
                 acc = bank(4 + 2 * h + u, [P, 2, HALF], "a_acc%d_%d" % (h, u))
                 for v in range(2):
@@ -159,25 +161,32 @@ def tile_picked_tokmax_none_po_kernel(
                     nc.scalar.activation(out=a_h[:, t, :], in_=acc[:, v, :], func=ACT.Copy, scale=g_abs[:, t : t + 1])
             return a_h
 
-        def gather_b(c0, width, name):
-            bq = sb([P, PACK, width], F32, name)
+        def gather_b(bq, c0):
+            width = bq.shape[2]
             for t in range(PACK):
                 nc.vector.tensor_copy(bq[:, t, :], b_sb[t][:].indirect(fl_t[:, c0 // 16 : (c0 + width) // 16]))
-            return bq
 
         def walk(ap):
             return ap.rearrange("p t (c i) -> p c t i", i=LINE)
 
         def larger(c, a_ap, bq_ap):
+            zp = sb([P, PACK, CHUNK], BF16, "zp%d" % c)
+            nc.vector.tensor_tensor(out=zp[:], in0=a_ap, in1=bq_ap, op=ALU.max)
+            return zp
+
+        def interleave(c, zp):
             zu = sb([P, CHUNK * PACK], BF16, "zu%d" % c)
-            nc.vector.tensor_tensor(
-                out=zu[:].rearrange("p (c i t) -> p c t i", i=LINE, t=PACK), in0=walk(a_ap), in1=walk(bq_ap), op=ALU.max
-            )
+            nc.vector.tensor_copy(out=zu[:].rearrange("p (c i t) -> p c t i", i=LINE, t=PACK), in_=walk(zp[:]))
             return zu
 
         def signed(c, zu):
             z = sb([P, CHUNK * PACK], BF16, "z%d" % c)
-            nc.vector.tensor_tensor(out=z[:], in0=zu[:], in1=g_sign[:].rearrange("p n t -> p (n t)"), op=ALU.mult)
+            nc.vector.tensor_tensor(
+                out=z[:].rearrange("p (n t) -> p n t", t=PACK),
+                in0=zu[:].rearrange("p (n t) -> p n t", t=PACK),
+                in1=g_sign[:].unsqueeze(1).to_broadcast([P, CHUNK, PACK]),
+                op=ALU.mult,
+            )
             return z
 
         def quantize_z(c, z):
@@ -206,7 +215,10 @@ def tile_picked_tokmax_none_po_kernel(
                     mix(acc[:, t, :], t, z_c, z_s)
                 nc.scalar.copy(out=y[:], in_=acc[:])
                 nc.sync.dma_start(out=out_v[:, :, cols], in_=y[:])
-                nc.scalar.copy(out=yg[:].rearrange("p (n t) -> p n t", t=PACK), in_=acc[:].rearrange("p t n -> p n t"))
+                if c < CHUNKS - 2:
+                    nc.scalar.copy(out=yg[:].rearrange("p (n t) -> p n t", t=PACK), in_=acc[:].rearrange("p t n -> p n t"))
+                else:
+                    nc.vector.tensor_copy(out=yg[:].rearrange("p (c i t) -> p c t i", i=LINE, t=PACK), in_=walk(y[:]))
             else:
                 accs = [bank(3 + u, [P, 2, CHUNK], "y_acc%d_%d" % (c, u)) for u in range(2)]
                 for t in range(PACK):
@@ -223,34 +235,29 @@ def tile_picked_tokmax_none_po_kernel(
             quantize(y_c[:], y_s[:, cols], yg[:])
             nc.sync.dma_start(out=words_v[:, cols], in_=y_c[:])
 
-        a0 = project_a(0)
         cast_half(wa_raw[1], wa_g[1][:])
-        bq01 = gather_b(0, HALF, "bq01")
-        w1s_d = deal_bytes(w1s, "w1s_d")
+        a0 = project_a(0)
+        bq01 = sb([P, PACK, HALF], BF16, "bq01")
+        bq2 = sb([P, PACK, CHUNK], BF16, "bq2")
+        gather_b(bq01, 0)
+        gather_b(bq2, 2 * CHUNK)
         quantize(wa_c[1][:], wa_s[1][:], wa_g[1][:])
         a1 = project_a(1)
-        bq2 = gather_b(2 * CHUNK, CHUNK, "bq2")
-        zu0 = larger(0, a0[:, :, 0:CHUNK], bq01[:, :, 0:CHUNK])
-        zu1 = larger(1, a0[:, :, CHUNK:HALF], bq01[:, :, CHUNK:HALF])
-        z0 = signed(0, zu0)
-        z1 = signed(1, zu1)
-        q0 = quantize_z(0, z0)
-        q1 = quantize_z(1, z1)
-        yg0 = mix_chunk(0, *q0)
-        yg1 = mix_chunk(1, *q1)
-        zu2 = larger(2, a1[:, :, 0:CHUNK], bq2[:])
-        bq3 = gather_b(3 * CHUNK, CHUNK, "bq3")
-        z2 = signed(2, zu2)
-        zu3 = larger(3, a1[:, :, CHUNK:HALF], bq3[:])
-        q2 = quantize_z(2, z2)
-        z3 = signed(3, zu3)
-        yg2 = mix_chunk(2, *q2)
-        planes(0, yg0)
-        q3 = quantize_z(3, z3)
-        planes(1, yg1)
-        yg3 = mix_chunk(3, *q3)
-        planes(2, yg2)
-        planes(3, yg3)
+        w1s_d = deal_bytes(w1s, "w1s_d")
+        bq3 = keep.tile([P, PACK, CHUNK], BF16, name="bq3", tag="late", align_bytes=64)
+        gather_b(bq3, 3 * CHUNK)
+        pairs = (
+            ((0, a0[:, :, 0:CHUNK], bq01[:, :, 0:CHUNK]), (1, a0[:, :, CHUNK:HALF], bq01[:, :, CHUNK:HALF])),
+            ((2, a1[:, :, 0:CHUNK], bq2[:]), (3, a1[:, :, CHUNK:HALF], bq3[:])),
+        )
+        yg = []
+        for pair in pairs:
+            zp = [larger(c, a_ap, bq_ap) for c, a_ap, bq_ap in pair]
+            zu = [interleave(c, zp[i]) for i, (c, a_ap, bq_ap) in enumerate(pair)]
+            z = [signed(c, zu[i]) for i, (c, a_ap, bq_ap) in enumerate(pair)]
+            zq = [quantize_z(c, z[i]) for i, (c, a_ap, bq_ap) in enumerate(pair)]
+            yg = yg + [mix_chunk(c, *zq[i]) for i, (c, a_ap, bq_ap) in enumerate(pair)]
+        for c in range(CHUNKS):
+            planes(c, yg[c])
         for q in range(4):
-            eng = nc.scalar if q % 2 else nc.sync
-            eng.dma_start(out=out_2[0, 4 * q : 4 * q + 4, :].bitcast(I32), in_=y_s[32 * q : 32 * q + 4, :].bitcast(I32))
+            nc.scalar.dma_start(out=out_2[0, 4 * q : 4 * q + 4, :].bitcast(I32), in_=y_s[32 * q : 32 * q + 4, :].bitcast(I32))

@@ -46,8 +46,11 @@ def tile_picked_tokmax_none_po_kernel(
         w1w = sb([P, 2 * N], U8, "w1w")
         w1s = sb([P, N], U8, "w1s")
         g = sb([P, PACK], F32, "g")
-        wb_raw = [sb([P, PACK, HALF], F32, "wb_raw%d" % h) for h in range(2)]
-        wa_raw = [sb([P, PACK, HALF], F32, "wa_raw%d" % h) for h in range(2)]
+        wb_raw = sb([P, PACK, H], F32, "wb_raw")
+        wa_raw = [
+            sb([P, PACK, HALF], F32, "wa_raw0"),
+            keep.tile([P, PACK, HALF], F32, name="wa_raw1", tag="a_sb0", align_bytes=64),
+        ]
 
         nc.vector.memset(xs[:].bitcast(I32), 0)
         nc.vector.memset(w1s[:].bitcast(I32), 0)
@@ -60,10 +63,9 @@ def tile_picked_tokmax_none_po_kernel(
 
         nc.sync.dma_start(out=w1w[:].bitcast(I32), in_=w1_words[0].bitcast(I32))
         nc.sync.dma_start(two_t[:], two)
-        nc.sync.dma_start(out=wb_raw[0][:], in_=wb_v[:, :, 0:HALF])
-        load_scale_rows(xs, x_scales)
-        nc.sync.dma_start(out=wb_raw[1][:], in_=wb_v[:, :, HALF:H])
         nc.sync.dma_start(offs_t[:], offs)
+        load_scale_rows(xs, x_scales)
+        nc.sync.dma_start(out=wb_raw[:], in_=wb_v)
         nc.sync.dma_start(out=xw[:], in_=x_words[0].rearrange("p n t -> p (n t)").bitcast(I32))
         nc.sync.dma_start(out=wa_raw[0][:], in_=wa_v[:, :, 0:HALF])
         nc.sync.dma_start(out=g[:], in_=gt.rearrange("(p t) o -> p (t o)", t=PACK))
@@ -71,11 +73,14 @@ def tile_picked_tokmax_none_po_kernel(
         nc.sync.dma_start(out=wa_raw[1][:], in_=wa_v[:, :, HALF:H])
         load_scale_rows(w1s, w1_scales)
 
-        def cast_half(raw, grouped):
-            nc.scalar.copy(
+        def cast(copy, raw, grouped):
+            copy(
                 out=grouped.rearrange("p (c i j) -> p c j i", i=LINE, j=PACK),
-                in_=raw[:].rearrange("p j (c i) -> p c j i", i=LINE),
+                in_=raw.rearrange("p j (c i) -> p c j i", i=LINE),
             )
+
+        def cast_half(raw, grouped):
+            cast(nc.scalar.copy, raw[:], grouped)
 
         def quantize(codes, scales, values):
             nc.vector.quantize_mx(out=codes.bitcast(FP8X4), scales=scales, in_=values)
@@ -93,8 +98,8 @@ def tile_picked_tokmax_none_po_kernel(
             )
             return dealt
 
-        def gather_words(lst, name):
-            dealt = sb([P, S], U32, name)
+        def gather_words(lst, name, tag):
+            dealt = keep.tile([P, S], U32, name=name, tag=tag, align_bytes=64)
             nc.vector.tensor_copy(dealt[:].rearrange("p (t m) -> p m t", t=PACK), xw[:].bitcast(U32).indirect(lst[:]))
             return dealt
 
@@ -108,7 +113,7 @@ def tile_picked_tokmax_none_po_kernel(
         xb_s = deal_bytes(sb_plain, "xb_s")
         xa_s = deal_bytes(sa_plain, "xa_s")
 
-        wb_g = sb([P, H * PACK], BF16, "wb_g")
+        wb_g = [keep.tile([P, HALF * PACK], BF16, name="wb_g%d" % h, tag="early%d" % h, align_bytes=64) for h in range(2)]
         wa_g = [
             sb([P, HALF * PACK], BF16, "wa_g0"),
             keep.tile([P, HALF * PACK], BF16, name="wa_g1", tag="late", align_bytes=64),
@@ -118,11 +123,12 @@ def tile_picked_tokmax_none_po_kernel(
         wa_c = [sb([P, HALF], U32, "wa_c%d" % h) for h in range(2)]
         wa_s = [sb([P, HALF], U8, "wa_s%d" % h) for h in range(2)]
 
+        cast(nc.scalar.copy, wb_raw[:, :, 0:HALF], wb_g[0][:])
+        cast(nc.vector.tensor_copy, wb_raw[:, :, HALF:H], wb_g[1][:])
         for h in range(2):
-            cast_half(wb_raw[h], wb_g[:, h * HALF * PACK : (h + 1) * HALF * PACK])
-        quantize(wb_c[:], wb_s[:], wb_g[:])
-        xb_w = gather_words(two_t, "xb_w")
-        xa_w = gather_words(offs_t, "xa_w")
+            quantize(wb_c[:, h * HALF : (h + 1) * HALF], wb_s[:, h * HALF : (h + 1) * HALF], wb_g[h][:])
+        xb_w = gather_words(two_t, "xb_w", "xb_w")
+        xa_w = gather_words(offs_t, "xa_w", "early0")
 
         def rows(t):
             return slice(t * P, (t + 1) * P)
@@ -174,9 +180,9 @@ def tile_picked_tokmax_none_po_kernel(
             nc.vector.tensor_tensor(out=zp[:], in0=a_ap, in1=bq_ap, op=ALU.max)
             return zp
 
-        def interleave(c, zp):
+        def interleave(c, zp, copy):
             zu = sb([P, CHUNK * PACK], BF16, "zu%d" % c)
-            nc.vector.tensor_copy(out=zu[:].rearrange("p (c i t) -> p c t i", i=LINE, t=PACK), in_=walk(zp[:]))
+            copy(out=zu[:].rearrange("p (c i t) -> p c t i", i=LINE, t=PACK), in_=walk(zp[:]))
             return zu
 
         def signed(c, zu):
@@ -204,36 +210,28 @@ def tile_picked_tokmax_none_po_kernel(
         out_v = out_0.rearrange("(p t) j -> p t j", t=PACK)
         words_v = out_1[0].rearrange("p n r -> p (n r)").bitcast(I32)
         y_s = sb([P, H], U8, "y_s")
+        y_c = sb([P, H], I32, "y_c")
 
         def mix_chunk(c, z_c, z_s):
-            cols = slice(c * CHUNK, (c + 1) * CHUNK)
             y = sb([P, PACK, CHUNK], F32, "y%d" % c)
+            parts = 2 if c == CHUNKS - 1 else 1
+            per = PACK // parts
+            for u in range(parts):
+                acc = bank(c + u, [P, per, CHUNK], "y_acc%d_%d" % (c, u))
+                for v in range(per):
+                    mix(acc[:, v, :], u * per + v, z_c, z_s)
+                nc.scalar.copy(out=y[:, u * per : (u + 1) * per, :], in_=acc[:])
+            nc.sync.dma_start(out=out_v[:, :, c * CHUNK : (c + 1) * CHUNK], in_=y[:])
+            return y
+
+        def round_y(c, y):
             yg = sb([P, CHUNK * PACK], BF16, "yg%d" % c)
-            if c < CHUNKS - 1:
-                acc = bank(c, [P, PACK, CHUNK], "y_acc%d" % c)
-                for t in range(PACK):
-                    mix(acc[:, t, :], t, z_c, z_s)
-                nc.scalar.copy(out=y[:], in_=acc[:])
-                nc.sync.dma_start(out=out_v[:, :, cols], in_=y[:])
-                if c < CHUNKS - 2:
-                    nc.scalar.copy(out=yg[:].rearrange("p (n t) -> p n t", t=PACK), in_=acc[:].rearrange("p t n -> p n t"))
-                else:
-                    nc.vector.tensor_copy(out=yg[:].rearrange("p (c i t) -> p c t i", i=LINE, t=PACK), in_=walk(y[:]))
-            else:
-                accs = [bank(3 + u, [P, 2, CHUNK], "y_acc%d_%d" % (c, u)) for u in range(2)]
-                for t in range(PACK):
-                    mix(accs[t // 2][:, t % 2, :], t, z_c, z_s)
-                nc.scalar.copy(out=y[:, 0:2, :], in_=accs[0][:])
-                nc.vector.tensor_copy(out=y[:, 2:4, :], in_=accs[1][:])
-                nc.sync.dma_start(out=out_v[:, :, cols], in_=y[:])
-                nc.vector.tensor_copy(out=yg[:].rearrange("p (c i t) -> p c t i", i=LINE, t=PACK), in_=walk(y[:]))
+            nc.vector.tensor_copy(out=yg[:].rearrange("p (c i t) -> p c t i", i=LINE, t=PACK), in_=walk(y[:]))
             return yg
 
         def planes(c, yg):
             cols = slice(c * CHUNK, (c + 1) * CHUNK)
-            y_c = sb([P, CHUNK], I32, "y_c%d" % c)
-            quantize(y_c[:], y_s[:, cols], yg[:])
-            nc.sync.dma_start(out=words_v[:, cols], in_=y_c[:])
+            quantize(y_c[:, cols], y_s[:, cols], yg[:])
 
         cast_half(wa_raw[1], wa_g[1][:])
         a0 = project_a(0)
@@ -243,21 +241,34 @@ def tile_picked_tokmax_none_po_kernel(
         gather_b(bq2, 2 * CHUNK)
         quantize(wa_c[1][:], wa_s[1][:], wa_g[1][:])
         a1 = project_a(1)
-        w1s_d = deal_bytes(w1s, "w1s_d")
         bq3 = keep.tile([P, PACK, CHUNK], BF16, name="bq3", tag="late", align_bytes=64)
         gather_b(bq3, 3 * CHUNK)
-        pairs = (
-            ((0, a0[:, :, 0:CHUNK], bq01[:, :, 0:CHUNK]), (1, a0[:, :, CHUNK:HALF], bq01[:, :, CHUNK:HALF])),
-            ((2, a1[:, :, 0:CHUNK], bq2[:]), (3, a1[:, :, CHUNK:HALF], bq3[:])),
-        )
-        yg = []
-        for pair in pairs:
-            zp = [larger(c, a_ap, bq_ap) for c, a_ap, bq_ap in pair]
-            zu = [interleave(c, zp[i]) for i, (c, a_ap, bq_ap) in enumerate(pair)]
-            z = [signed(c, zu[i]) for i, (c, a_ap, bq_ap) in enumerate(pair)]
-            zq = [quantize_z(c, z[i]) for i, (c, a_ap, bq_ap) in enumerate(pair)]
-            yg = yg + [mix_chunk(c, *zq[i]) for i, (c, a_ap, bq_ap) in enumerate(pair)]
-        for c in range(CHUNKS):
-            planes(c, yg[c])
+        w1s_d = deal_bytes(w1s, "w1s_d")
+        zp0 = larger(0, a0[:, :, 0:CHUNK], bq01[:, :, 0:CHUNK])
+        zp1 = larger(1, a0[:, :, CHUNK:HALF], bq01[:, :, CHUNK:HALF])
+        zu0 = interleave(0, zp0, nc.scalar.copy)
+        zu1 = interleave(1, zp1, nc.scalar.copy)
+        zp2 = larger(2, a1[:, :, 0:CHUNK], bq2[:])
+        zp3 = larger(3, a1[:, :, CHUNK:HALF], bq3[:])
+        z0 = signed(0, zu0)
+        zu2 = interleave(2, zp2, nc.vector.tensor_copy)
+        y0 = mix_chunk(0, *quantize_z(0, z0))
+        z1 = signed(1, zu1)
+        z2 = signed(2, zu2)
+        y1 = mix_chunk(1, *quantize_z(1, z1))
+        zu3 = interleave(3, zp3, nc.vector.tensor_copy)
+        y2 = mix_chunk(2, *quantize_z(2, z2))
+        z3 = signed(3, zu3)
+        yg0 = round_y(0, y0)
+        y3 = mix_chunk(3, *quantize_z(3, z3))
+        yg1 = round_y(1, y1)
+        planes(0, yg0)
+        yg2 = round_y(2, y2)
+        planes(1, yg1)
+        planes(2, yg2)
+        nc.sync.dma_start(out=words_v[:, 0 : 3 * CHUNK], in_=y_c[:, 0 : 3 * CHUNK])
+        planes(3, round_y(3, y3))
+        nc.sync.dma_start(out=words_v[:, 3 * CHUNK : H], in_=y_c[:, 3 * CHUNK : H])
         for q in range(4):
-            nc.scalar.dma_start(out=out_2[0, 4 * q : 4 * q + 4, :].bitcast(I32), in_=y_s[32 * q : 32 * q + 4, :].bitcast(I32))
+            eng = nc.scalar if q % 2 else nc.sync
+            eng.dma_start(out=out_2[0, 4 * q : 4 * q + 4, :].bitcast(I32), in_=y_s[32 * q : 32 * q + 4, :].bitcast(I32))

@@ -57,21 +57,21 @@ def tile_picked_tokmax_none_po_kernel(
 
         wb_v = wb.rearrange("(p j) c -> p j c", j=PACK)
         wa_v = wa.rearrange("(p j) c -> p j c", j=PACK)
-        def load_scale_rows(dst, src):
+        def load_scale_rows(dst, src, queues):
             for q in range(4):
-                nc.sync.dma_start(out=dst[32 * q : 32 * q + 4, :].bitcast(I32), in_=src[0, 4 * q : 4 * q + 4, :].bitcast(I32))
+                queues[q].dma_start(out=dst[32 * q : 32 * q + 4, :].bitcast(I32), in_=src[0, 4 * q : 4 * q + 4, :].bitcast(I32))
 
         nc.sync.dma_start(out=w1w[:].bitcast(I32), in_=w1_words[0].bitcast(I32))
         nc.sync.dma_start(two_t[:], two)
         nc.sync.dma_start(offs_t[:], offs)
-        load_scale_rows(xs, x_scales)
+        load_scale_rows(xs, x_scales, (nc.sync, nc.sync, nc.scalar, nc.scalar))
         nc.sync.dma_start(out=wb_raw[:], in_=wb_v)
+        load_scale_rows(w1s, w1_scales, (nc.sync,) * 4)
         nc.sync.dma_start(out=xw[:], in_=x_words[0].rearrange("p n t -> p (n t)").bitcast(I32))
         nc.sync.dma_start(out=wa_raw[0][:], in_=wa_v[:, :, 0:HALF])
         nc.sync.dma_start(out=g[:], in_=gt.rearrange("(p t) o -> p (t o)", t=PACK))
         nc.sync.dma_start(fl_t[:], fl)
         nc.sync.dma_start(out=wa_raw[1][:], in_=wa_v[:, :, HALF:H])
-        load_scale_rows(w1s, w1_scales)
 
         def cast(copy, raw, grouped):
             copy(
@@ -85,16 +85,11 @@ def tile_picked_tokmax_none_po_kernel(
         def quantize(codes, scales, values):
             nc.vector.quantize_mx(out=codes.bitcast(FP8X4), scales=scales, in_=values)
 
-        def gather_scales(lst, name):
-            plain = sb([P, S], U8, name + "_plain")
-            nc.vector.tensor_copy(plain[:], xs[:].indirect(lst[:]))
-            return plain
-
         def deal_bytes(plain, name):
-            dealt = sb([P, S], U8, name)
+            dealt = sb([P, plain.shape[1]], U8, name)
             nc.vector.tensor_copy(
-                out=dealt[:].rearrange("p (t m) -> p t m", t=PACK),
-                in_=plain[:].rearrange("p (m t) -> p t m", t=PACK),
+                out=dealt[:].rearrange("p (l t m) -> p l t m", t=PACK, m=P),
+                in_=plain[:].rearrange("p (l m t) -> p l t m", t=PACK, m=P),
             )
             return dealt
 
@@ -108,10 +103,12 @@ def tile_picked_tokmax_none_po_kernel(
             out=w1w_d[:].rearrange("p (t m b) -> p t m b", t=PACK, b=2),
             in_=w1w[:].rearrange("p (m t b) -> p t m b", t=PACK, b=2),
         )
-        sb_plain = gather_scales(two_t, "xb_s")
-        sa_plain = gather_scales(offs_t, "xa_s")
-        xb_s = deal_bytes(sb_plain, "xb_s")
-        xa_s = deal_bytes(sa_plain, "xa_s")
+        picked_s = sb([P, 2 * S], U8, "picked_s")
+        nc.vector.tensor_copy(picked_s[:, 0:S], xs[:].indirect(two_t[:]))
+        nc.vector.tensor_copy(picked_s[:, S : 2 * S], xs[:].indirect(offs_t[:]))
+        w1s_d = deal_bytes(w1s, "w1s_d")
+        x_s = deal_bytes(picked_s, "x_s")
+        xb_s, xa_s = x_s[:, 0:S], x_s[:, S : 2 * S]
 
         wb_g = [keep.tile([P, HALF * PACK], BF16, name="wb_g%d" % h, tag="early%d" % h, align_bytes=64) for h in range(2)]
         wa_g = [
@@ -124,11 +121,12 @@ def tile_picked_tokmax_none_po_kernel(
         wa_s = [sb([P, HALF], U8, "wa_s%d" % h) for h in range(2)]
 
         cast(nc.scalar.copy, wb_raw[:, :, 0:HALF], wb_g[0][:])
-        cast(nc.vector.tensor_copy, wb_raw[:, :, HALF:H], wb_g[1][:])
+        cast(nc.scalar.copy, wb_raw[:, :, HALF : HALF + CHUNK], wb_g[1][:, 0 : CHUNK * PACK])
+        cast(nc.vector.tensor_copy, wb_raw[:, :, HALF + CHUNK : H], wb_g[1][:, CHUNK * PACK : HALF * PACK])
         for h in range(2):
             quantize(wb_c[:, h * HALF : (h + 1) * HALF], wb_s[:, h * HALF : (h + 1) * HALF], wb_g[h][:])
         xb_w = gather_words(two_t, "xb_w", "xb_w")
-        xa_w = gather_words(offs_t, "xa_w", "early0")
+        xa_w = gather_words(offs_t, "xa_w", "early1")
 
         def rows(t):
             return slice(t * P, (t + 1) * P)
@@ -167,22 +165,18 @@ def tile_picked_tokmax_none_po_kernel(
                     nc.scalar.activation(out=a_h[:, t, :], in_=acc[:, v, :], func=ACT.Copy, scale=g_abs[:, t : t + 1])
             return a_h
 
-        def gather_b(bq, c0):
-            width = bq.shape[2]
-            for t in range(PACK):
-                nc.vector.tensor_copy(bq[:, t, :], b_sb[t][:].indirect(fl_t[:, c0 // 16 : (c0 + width) // 16]))
+        def gather_b(bq_ap, t, h):
+            nc.vector.tensor_copy(bq_ap, b_sb[t][:].indirect(fl_t[:, h * HALF // 16 : (h + 1) * HALF // 16]))
 
         def walk(ap):
             return ap.rearrange("p t (c i) -> p c t i", i=LINE)
 
-        def larger(c, a_ap, bq_ap):
-            zp = sb([P, PACK, CHUNK], BF16, "zp%d" % c)
-            nc.vector.tensor_tensor(out=zp[:], in0=a_ap, in1=bq_ap, op=ALU.max)
-            return zp
+        def larger(zp_ap, a_ap, bq_ap):
+            nc.vector.tensor_tensor(out=zp_ap, in0=a_ap, in1=bq_ap, op=ALU.max)
 
         def interleave(c, zp, copy):
             zu = sb([P, CHUNK * PACK], BF16, "zu%d" % c)
-            copy(out=zu[:].rearrange("p (c i t) -> p c t i", i=LINE, t=PACK), in_=walk(zp[:]))
+            copy(out=zu[:].rearrange("p (c i t) -> p c t i", i=LINE, t=PACK), in_=walk(zp))
             return zu
 
         def signed(c, zu):
@@ -235,32 +229,34 @@ def tile_picked_tokmax_none_po_kernel(
 
         cast_half(wa_raw[1], wa_g[1][:])
         a0 = project_a(0)
-        bq01 = sb([P, PACK, HALF], BF16, "bq01")
-        bq2 = sb([P, PACK, CHUNK], BF16, "bq2")
-        gather_b(bq01, 0)
-        gather_b(bq2, 2 * CHUNK)
+        bq0 = sb([P, PACK, HALF], BF16, "bq0")
+        bq1_low = sb([P, 1, HALF], BF16, "bq1_low")
+        for t in range(PACK):
+            gather_b(bq0[:, t, :], t, 0)
+        gather_b(bq1_low[:, 0, :], 0, 1)
         quantize(wa_c[1][:], wa_s[1][:], wa_g[1][:])
         a1 = project_a(1)
-        bq3 = keep.tile([P, PACK, CHUNK], BF16, name="bq3", tag="late", align_bytes=64)
-        gather_b(bq3, 3 * CHUNK)
-        w1s_d = deal_bytes(w1s, "w1s_d")
-        zp0 = larger(0, a0[:, :, 0:CHUNK], bq01[:, :, 0:CHUNK])
-        zp1 = larger(1, a0[:, :, CHUNK:HALF], bq01[:, :, CHUNK:HALF])
-        zu0 = interleave(0, zp0, nc.scalar.copy)
-        zu1 = interleave(1, zp1, nc.scalar.copy)
-        zp2 = larger(2, a1[:, :, 0:CHUNK], bq2[:])
-        zp3 = larger(3, a1[:, :, CHUNK:HALF], bq3[:])
+        bq1_high = keep.tile([P, PACK - 1, HALF], BF16, name="bq1_high", tag="late", align_bytes=64)
+        for t in range(1, PACK):
+            gather_b(bq1_high[:, t - 1, :], t, 1)
+        zp01 = sb([P, PACK, HALF], BF16, "zp01")
+        zp23 = sb([P, PACK, HALF], BF16, "zp23")
+        larger(zp01[:], a0[:], bq0[:])
+        zu1 = interleave(1, zp01[:, :, CHUNK:HALF], nc.scalar.copy)
+        larger(zp23[:, 0:1, :], a1[:, 0:1, :], bq1_low[:])
+        zu0 = interleave(0, zp01[:, :, 0:CHUNK], nc.vector.tensor_copy)
+        larger(zp23[:, 1:4, :], a1[:, 1:4, :], bq1_high[:])
         z0 = signed(0, zu0)
-        zu2 = interleave(2, zp2, nc.vector.tensor_copy)
+        zu2 = interleave(2, zp23[:, :, 0:CHUNK], nc.scalar.copy)
+        zu3 = interleave(3, zp23[:, :, CHUNK:HALF], nc.scalar.copy)
         y0 = mix_chunk(0, *quantize_z(0, z0))
         z1 = signed(1, zu1)
         z2 = signed(2, zu2)
         y1 = mix_chunk(1, *quantize_z(1, z1))
-        zu3 = interleave(3, zp3, nc.vector.tensor_copy)
-        y2 = mix_chunk(2, *quantize_z(2, z2))
         z3 = signed(3, zu3)
-        yg0 = round_y(0, y0)
+        y2 = mix_chunk(2, *quantize_z(2, z2))
         y3 = mix_chunk(3, *quantize_z(3, z3))
+        yg0 = round_y(0, y0)
         yg1 = round_y(1, y1)
         planes(0, yg0)
         yg2 = round_y(2, y2)

@@ -236,6 +236,12 @@ def tile_picked_tokmax_none_po_kernel(
         gather_b(bq1_low[:, 0, :], 0, 1)
         quantize(wa_c[1][:], wa_s[1][:], wa_g[1][:])
         a1 = project_a(1)
+        warm = bank(7, [P, H], "warm")
+        for t in range(3):
+            nc.tensor.matmul_mx(
+                out=warm[:], lhsT=xb_w[:, rows(t)].bitcast(FP8X4), lhsT_scale=xb_s[:, rows(t)],
+                rhs=wb_c[:].bitcast(FP8X4), rhs_scale=wb_s[:], start=True, stop=True,
+            )
         bq1_high = keep.tile([P, PACK - 1, HALF], BF16, name="bq1_high", tag="late", align_bytes=64)
         for t in range(1, PACK):
             gather_b(bq1_high[:, t - 1, :], t, 1)

@@ -22,6 +22,7 @@ HALF = H // 2
 CHUNK = 128
 CHUNKS = H // CHUNK
 LINE = 4
+WARMUPS = 2
 
 
 def tile_picked_tokmax_none_po_kernel(
@@ -57,6 +58,7 @@ def tile_picked_tokmax_none_po_kernel(
 
         wb_v = wb.rearrange("(p j) c -> p j c", j=PACK)
         wa_v = wa.rearrange("(p j) c -> p j c", j=PACK)
+
         def load_scale_rows(dst, src, queues):
             for q in range(4):
                 queues[q].dma_start(out=dst[32 * q : 32 * q + 4, :].bitcast(I32), in_=src[0, 4 * q : 4 * q + 4, :].bitcast(I32))
@@ -78,9 +80,6 @@ def tile_picked_tokmax_none_po_kernel(
                 out=grouped.rearrange("p (c i j) -> p c j i", i=LINE, j=PACK),
                 in_=raw.rearrange("p j (c i) -> p c j i", i=LINE),
             )
-
-        def cast_half(raw, grouped):
-            cast(nc.scalar.copy, raw[:], grouped)
 
         def quantize(codes, scales, values):
             nc.vector.quantize_mx(out=codes.bitcast(FP8X4), scales=scales, in_=values)
@@ -131,7 +130,7 @@ def tile_picked_tokmax_none_po_kernel(
         def rows(t):
             return slice(t * P, (t + 1) * P)
 
-        cast_half(wa_raw[0], wa_g[0][:])
+        cast(nc.scalar.copy, wa_raw[0][:], wa_g[0][:])
         quantize(wa_c[0][:], wa_s[0][:], wa_g[0][:])
 
         g_abs = sb([P, PACK], F32, "g_abs")
@@ -139,13 +138,16 @@ def tile_picked_tokmax_none_po_kernel(
         nc.scalar.activation(out=g_abs[:], in_=g[:], func=ACT.Abs)
         nc.scalar.activation(out=g_sign[:], in_=g[:], func=ACT.Sign)
 
-        b_sb = []
-        for t in range(PACK):
-            acc = bank(t, [P, H], "b_acc%d" % t)
+        def project_b(acc, t):
             nc.tensor.matmul_mx(
                 out=acc[:], lhsT=xb_w[:, rows(t)].bitcast(FP8X4), lhsT_scale=xb_s[:, rows(t)],
                 rhs=wb_c[:].bitcast(FP8X4), rhs_scale=wb_s[:], start=True, stop=True,
             )
+
+        b_sb = []
+        for t in range(PACK):
+            acc = bank(t, [P, H], "b_acc%d" % t)
+            project_b(acc, t)
             b_t = sb([P, H], F32, "b_sb%d" % t)
             nc.scalar.activation(out=b_t[:], in_=acc[:], func=ACT.Copy, scale=g_abs[:, t : t + 1])
             b_sb.append(b_t)
@@ -223,11 +225,11 @@ def tile_picked_tokmax_none_po_kernel(
             nc.vector.tensor_copy(out=yg[:].rearrange("p (c i t) -> p c t i", i=LINE, t=PACK), in_=walk(y[:]))
             return yg
 
-        def planes(c, yg):
+        def quantize_y(c, yg):
             cols = slice(c * CHUNK, (c + 1) * CHUNK)
             quantize(y_c[:, cols], y_s[:, cols], yg[:])
 
-        cast_half(wa_raw[1], wa_g[1][:])
+        cast(nc.scalar.copy, wa_raw[1][:], wa_g[1][:])
         a0 = project_a(0)
         bq0 = sb([P, PACK, HALF], BF16, "bq0")
         bq1_low = sb([P, 1, HALF], BF16, "bq1_low")
@@ -236,22 +238,22 @@ def tile_picked_tokmax_none_po_kernel(
         gather_b(bq1_low[:, 0, :], 0, 1)
         quantize(wa_c[1][:], wa_s[1][:], wa_g[1][:])
         a1 = project_a(1)
+
         warm = bank(7, [P, H], "warm")
-        for t in range(3):
-            nc.tensor.matmul_mx(
-                out=warm[:], lhsT=xb_w[:, rows(t)].bitcast(FP8X4), lhsT_scale=xb_s[:, rows(t)],
-                rhs=wb_c[:].bitcast(FP8X4), rhs_scale=wb_s[:], start=True, stop=True,
-            )
+        for t in range(WARMUPS):
+            project_b(warm, t)
+
         bq1_high = keep.tile([P, PACK - 1, HALF], BF16, name="bq1_high", tag="late", align_bytes=64)
         for t in range(1, PACK):
             gather_b(bq1_high[:, t - 1, :], t, 1)
+
         zp01 = sb([P, PACK, HALF], BF16, "zp01")
         zp23 = sb([P, PACK, HALF], BF16, "zp23")
         larger(zp01[:], a0[:], bq0[:])
         zu1 = interleave(1, zp01[:, :, CHUNK:HALF], nc.scalar.copy)
         larger(zp23[:, 0:1, :], a1[:, 0:1, :], bq1_low[:])
         zu0 = interleave(0, zp01[:, :, 0:CHUNK], nc.vector.tensor_copy)
-        larger(zp23[:, 1:4, :], a1[:, 1:4, :], bq1_high[:])
+        larger(zp23[:, 1:PACK, :], a1[:, 1:PACK, :], bq1_high[:])
         z0 = signed(0, zu0)
         zu2 = interleave(2, zp23[:, :, 0:CHUNK], nc.scalar.copy)
         zu3 = interleave(3, zp23[:, :, CHUNK:HALF], nc.scalar.copy)
@@ -264,13 +266,15 @@ def tile_picked_tokmax_none_po_kernel(
         y3 = mix_chunk(3, *quantize_z(3, z3))
         yg0 = round_y(0, y0)
         yg1 = round_y(1, y1)
-        planes(0, yg0)
+        quantize_y(0, yg0)
         yg2 = round_y(2, y2)
-        planes(1, yg1)
-        planes(2, yg2)
-        nc.sync.dma_start(out=words_v[:, 0 : 3 * CHUNK], in_=y_c[:, 0 : 3 * CHUNK])
-        planes(3, round_y(3, y3))
-        nc.sync.dma_start(out=words_v[:, 3 * CHUNK : H], in_=y_c[:, 3 * CHUNK : H])
+        quantize_y(1, yg1)
+        quantize_y(2, yg2)
+
+        last = H - CHUNK
+        nc.sync.dma_start(out=words_v[:, 0:last], in_=y_c[:, 0:last])
+        quantize_y(3, round_y(3, y3))
+        nc.sync.dma_start(out=words_v[:, last:H], in_=y_c[:, last:H])
         for q in range(4):
             eng = nc.scalar if q % 2 else nc.sync
             eng.dma_start(out=out_2[0, 4 * q : 4 * q + 4, :].bitcast(I32), in_=y_s[32 * q : 32 * q + 4, :].bitcast(I32))

@@ -50,7 +50,7 @@ def tile_picked_tokmax_none_po_kernel(
         wb_raw = sb([P, PACK, H], F32, "wb_raw")
         wa_raw = [
             sb([P, PACK, HALF], F32, "wa_raw0"),
-            keep.tile([P, PACK, HALF], F32, name="wa_raw1", tag="a_sb0", align_bytes=64),
+            sb([P, PACK, HALF], F32, "wa_raw1"),
         ]
 
         nc.vector.memset(xs[:].bitcast(I32), 0)
@@ -110,10 +110,7 @@ def tile_picked_tokmax_none_po_kernel(
         xb_s, xa_s = x_s[:, 0:S], x_s[:, S : 2 * S]
 
         wb_g = [keep.tile([P, HALF * PACK], BF16, name="wb_g%d" % h, tag="early%d" % h, align_bytes=64) for h in range(2)]
-        wa_g = [
-            sb([P, HALF * PACK], BF16, "wa_g0"),
-            keep.tile([P, HALF * PACK], BF16, name="wa_g1", tag="late", align_bytes=64),
-        ]
+        wa_g0 = keep.tile([P, HALF * PACK], BF16, name="wa_g0", tag="late", align_bytes=64)
         wb_c = sb([P, H], U32, "wb_c")
         wb_s = sb([P, H], U8, "wb_s")
         wa_c = [sb([P, HALF], U32, "wa_c%d" % h) for h in range(2)]
@@ -130,8 +127,13 @@ def tile_picked_tokmax_none_po_kernel(
         def rows(t):
             return slice(t * P, (t + 1) * P)
 
-        cast(nc.scalar.copy, wa_raw[0][:], wa_g[0][:])
-        quantize(wa_c[0][:], wa_s[0][:], wa_g[0][:])
+        cast(nc.scalar.copy, wa_raw[0][:], wa_g0[:])
+        quantize(wa_c[0][:], wa_s[0][:], wa_g0[:])
+        wa_g1 = keep.tile([P, HALF * PACK], BF16, name="wa_g1", tag="late", align_bytes=64)
+        nc.gpsimd.tensor_scalar(
+            out=wa_g1[:].rearrange("p (c j) -> p c j", j=PACK), in0=wa_raw[1][:].rearrange("p j c -> p c j"),
+            scalar1=1.0, scalar2=0.0, op0=ALU.mult, op1=ALU.add,
+        )
 
         g_abs = sb([P, PACK], F32, "g_abs")
         g_sign = sb([P, PACK], BF16, "g_sign")
@@ -229,14 +231,13 @@ def tile_picked_tokmax_none_po_kernel(
             cols = slice(c * CHUNK, (c + 1) * CHUNK)
             quantize(y_c[:, cols], y_s[:, cols], yg[:])
 
-        cast(nc.scalar.copy, wa_raw[1][:], wa_g[1][:])
         a0 = project_a(0)
         bq0 = sb([P, PACK, HALF], BF16, "bq0")
         bq1_low = sb([P, 1, HALF], BF16, "bq1_low")
         for t in range(PACK):
             gather_b(bq0[:, t, :], t, 0)
         gather_b(bq1_low[:, 0, :], 0, 1)
-        quantize(wa_c[1][:], wa_s[1][:], wa_g[1][:])
+        quantize(wa_c[1][:], wa_s[1][:], wa_g1[:])
         a1 = project_a(1)
 
         warm = bank(7, [P, H], "warm")

@@ -47,11 +47,10 @@ def tile_picked_tokmax_none_po_kernel(
         w1w = sb([P, 2 * N], U8, "w1w")
         w1s = sb([P, N], U8, "w1s")
         g = sb([P, PACK], F32, "g")
-        wb_raw = sb([P, PACK, H], F32, "wb_raw")
-        wa_raw = [
-            sb([P, PACK, HALF], F32, "wa_raw0"),
-            sb([P, PACK, HALF], F32, "wa_raw1"),
-        ]
+        wb_half = sb([P, PACK, HALF], F32, "wb_half")
+        wb_third = sb([P, PACK, CHUNK], F32, "wb_third")
+        wb_last = keep.tile([P, PACK, CHUNK], F32, name="wb_last", tag="wb_last", align_bytes=64)
+        wa_raw = [keep.tile([P, PACK, HALF], F32, name="wa_raw%d" % h, tag="wa_raw%d" % h, align_bytes=64) for h in range(2)]
 
         nc.vector.memset(xs[:].bitcast(I32), 0)
         nc.vector.memset(w1s[:].bitcast(I32), 0)
@@ -67,13 +66,15 @@ def tile_picked_tokmax_none_po_kernel(
         nc.sync.dma_start(two_t[:], two)
         nc.sync.dma_start(offs_t[:], offs)
         load_scale_rows(xs, x_scales, (nc.sync, nc.sync, nc.scalar, nc.scalar))
-        nc.sync.dma_start(out=wb_raw[:], in_=wb_v)
-        load_scale_rows(w1s, w1_scales, (nc.sync,) * 4)
         nc.sync.dma_start(out=xw[:], in_=x_words[0].rearrange("p n t -> p (n t)").bitcast(I32))
-        nc.sync.dma_start(out=wa_raw[0][:], in_=wa_v[:, :, 0:HALF])
+        load_scale_rows(w1s, w1_scales, (nc.sync,) * 4)
         nc.sync.dma_start(out=g[:], in_=gt.rearrange("(p t) o -> p (t o)", t=PACK))
+        nc.sync.dma_start(out=wb_half[:], in_=wb_v[:, :, 0:HALF])
+        nc.sync.dma_start(out=wb_third[:], in_=wb_v[:, :, HALF : HALF + CHUNK])
+        nc.sync.dma_start(out=wb_last[:], in_=wb_v[:, :, HALF + CHUNK : H])
         nc.sync.dma_start(fl_t[:], fl)
-        nc.sync.dma_start(out=wa_raw[1][:], in_=wa_v[:, :, HALF:H])
+        for h in range(2):
+            nc.sync.dma_start(out=wa_raw[h][:], in_=wa_v[:, :, h * HALF : (h + 1) * HALF])
 
         def cast(copy, raw, grouped):
             copy(
@@ -105,59 +106,65 @@ def tile_picked_tokmax_none_po_kernel(
         picked_s = sb([P, 2 * S], U8, "picked_s")
         nc.vector.tensor_copy(picked_s[:, 0:S], xs[:].indirect(two_t[:]))
         nc.vector.tensor_copy(picked_s[:, S : 2 * S], xs[:].indirect(offs_t[:]))
-        w1s_d = deal_bytes(w1s, "w1s_d")
         x_s = deal_bytes(picked_s, "x_s")
         xb_s, xa_s = x_s[:, 0:S], x_s[:, S : 2 * S]
-
-        wb_g = [keep.tile([P, HALF * PACK], BF16, name="wb_g%d" % h, tag="early%d" % h, align_bytes=64) for h in range(2)]
-        wa_g0 = keep.tile([P, HALF * PACK], BF16, name="wa_g0", tag="late", align_bytes=64)
-        wb_c = sb([P, H], U32, "wb_c")
-        wb_s = sb([P, H], U8, "wb_s")
-        wa_c = [sb([P, HALF], U32, "wa_c%d" % h) for h in range(2)]
-        wa_s = [sb([P, HALF], U8, "wa_s%d" % h) for h in range(2)]
-
-        cast(nc.scalar.copy, wb_raw[:, :, 0:HALF], wb_g[0][:])
-        cast(nc.scalar.copy, wb_raw[:, :, HALF : HALF + CHUNK], wb_g[1][:, 0 : CHUNK * PACK])
-        cast(nc.vector.tensor_copy, wb_raw[:, :, HALF + CHUNK : H], wb_g[1][:, CHUNK * PACK : HALF * PACK])
-        for h in range(2):
-            quantize(wb_c[:, h * HALF : (h + 1) * HALF], wb_s[:, h * HALF : (h + 1) * HALF], wb_g[h][:])
         xb_w = gather_words(two_t, "xb_w", "xb_w")
-        xa_w = gather_words(offs_t, "xa_w", "early1")
-
-        def rows(t):
-            return slice(t * P, (t + 1) * P)
-
-        cast(nc.scalar.copy, wa_raw[0][:], wa_g0[:])
-        quantize(wa_c[0][:], wa_s[0][:], wa_g0[:])
-        wa_g1 = keep.tile([P, HALF * PACK], BF16, name="wa_g1", tag="late", align_bytes=64)
-        nc.gpsimd.tensor_scalar(
-            out=wa_g1[:].rearrange("p (c j) -> p c j", j=PACK), in0=wa_raw[1][:].rearrange("p j c -> p c j"),
-            scalar1=1.0, scalar2=0.0, op0=ALU.mult, op1=ALU.add,
-        )
+        w1s_d = deal_bytes(w1s, "w1s_d")
 
         g_abs = sb([P, PACK], F32, "g_abs")
         g_sign = sb([P, PACK], BF16, "g_sign")
         nc.scalar.activation(out=g_abs[:], in_=g[:], func=ACT.Abs)
         nc.scalar.activation(out=g_sign[:], in_=g[:], func=ACT.Sign)
 
-        def project_b(acc, t):
-            nc.tensor.matmul_mx(
-                out=acc[:], lhsT=xb_w[:, rows(t)].bitcast(FP8X4), lhsT_scale=xb_s[:, rows(t)],
-                rhs=wb_c[:].bitcast(FP8X4), rhs_scale=wb_s[:], start=True, stop=True,
+        def cast_on_gpsimd(raw, grouped):
+            nc.gpsimd.tensor_scalar(
+                out=grouped.rearrange("p (c j) -> p c j", j=PACK), in0=raw.rearrange("p j c -> p c j"),
+                scalar1=1.0, scalar2=0.0, op0=ALU.mult, op1=ALU.add,
             )
 
-        b_sb = []
-        for t in range(PACK):
-            acc = bank(t, [P, H], "b_acc%d" % t)
-            project_b(acc, t)
-            b_t = sb([P, H], F32, "b_sb%d" % t)
-            nc.scalar.activation(out=b_t[:], in_=acc[:], func=ACT.Copy, scale=g_abs[:, t : t + 1])
-            b_sb.append(b_t)
+        def staged(name):
+            return keep.tile([P, HALF * PACK], BF16, name=name, tag="staged", align_bytes=64)
+
+        wb_g = [sb([P, HALF * PACK], BF16, "wb_g0"), staged("wb_g1")]
+        wb_c = sb([P, H], U32, "wb_c")
+        wb_s = sb([P, H], U8, "wb_s")
+        wa_c = [sb([P, HALF], U32, "wa_c%d" % h) for h in range(2)]
+        wa_s = [sb([P, HALF], U8, "wa_s%d" % h) for h in range(2)]
+        quarter = CHUNK * PACK
+        cast(nc.scalar.copy, wb_half[:, :, 0:CHUNK], wb_g[0][:, 0:quarter])
+        cast_on_gpsimd(wb_half[:, :, CHUNK:HALF], wb_g[0][:, quarter : 2 * quarter])
+        cast(nc.scalar.copy, wb_third[:], wb_g[1][:, 0:quarter])
+        cast(nc.scalar.copy, wb_last[:], wb_g[1][:, quarter : 2 * quarter])
+        for h in range(2):
+            quantize(wb_c[:, h * HALF : (h + 1) * HALF], wb_s[:, h * HALF : (h + 1) * HALF], wb_g[h][:])
+        xa_w = gather_words(offs_t, "xa_w", "wb_last")
+
+        def rows(t):
+            return slice(t * P, (t + 1) * P)
+
+        def project_b(acc, t, cols):
+            nc.tensor.matmul_mx(
+                out=acc, lhsT=xb_w[:, rows(t)].bitcast(FP8X4), lhsT_scale=xb_s[:, rows(t)],
+                rhs=wb_c[:, cols].bitcast(FP8X4), rhs_scale=wb_s[:, cols], start=True, stop=True,
+            )
+
+        b_sb = [sb([P, H], F32, "b_sb%d" % t) for t in range(PACK)]
+
+        def half_of_b(t, h):
+            cols = slice(h * HALF, (h + 1) * HALF)
+            acc = bank(PACK * h + t, [P, HALF], "b_acc%d_%d" % (t, h))
+            project_b(acc[:], t, cols)
+            nc.scalar.activation(out=b_sb[t][:, cols], in_=acc[:], func=ACT.Copy, scale=g_abs[:, t : t + 1])
+
+        for pair in range(2):
+            for h in range(2):
+                for t in (2 * pair, 2 * pair + 1):
+                    half_of_b(t, h)
 
         def project_a(h):
             a_h = sb([P, PACK, HALF], BF16, "a_sb%d" % h)
             for u in range(2):
-                acc = bank(4 + 2 * h + u, [P, 2, HALF], "a_acc%d_%d" % (h, u))
+                acc = bank(2 * h + u, [P, 2, HALF], "a_acc%d_%d" % (h, u))
                 for v in range(2):
                     t = 2 * u + v
                     nc.tensor.matmul_mx(
@@ -215,7 +222,7 @@ def tile_picked_tokmax_none_po_kernel(
             parts = 2 if c == CHUNKS - 1 else 1
             per = PACK // parts
             for u in range(parts):
-                acc = bank(c + u, [P, per, CHUNK], "y_acc%d_%d" % (c, u))
+                acc = bank(3 + (1 + c + u) % 5, [P, per, CHUNK], "y_acc%d_%d" % (c, u))
                 for v in range(per):
                     mix(acc[:, v, :], u * per + v, z_c, z_s)
                 nc.scalar.copy(out=y[:, u * per : (u + 1) * per, :], in_=acc[:])
@@ -231,37 +238,46 @@ def tile_picked_tokmax_none_po_kernel(
             cols = slice(c * CHUNK, (c + 1) * CHUNK)
             quantize(y_c[:, cols], y_s[:, cols], yg[:])
 
+        bq0 = [keep.tile([P, 2, HALF], BF16, name="bq0_0", tag="bq0_0", align_bytes=64)[:], None]
+        for t in range(2):
+            gather_b(bq0[0][:, t, :], t, 0)
+        wa_g0 = staged("wa_g0")
+        cast_on_gpsimd(wa_raw[0][:], wa_g0[:])
+        quantize(wa_c[0][:], wa_s[0][:], wa_g0[:])
         a0 = project_a(0)
-        bq0 = sb([P, PACK, HALF], BF16, "bq0")
-        bq1_low = sb([P, 1, HALF], BF16, "bq1_low")
-        for t in range(PACK):
-            gather_b(bq0[:, t, :], t, 0)
+        held = keep.tile([P, 3, HALF], BF16, name="held", tag="wa_raw0", align_bytes=64)
+        bq0[1] = held[:, 0:2, :]
+        for t in range(2, PACK):
+            gather_b(bq0[1][:, t - 2, :], t, 0)
+        bq1_low = held[:, 2:3, :]
         gather_b(bq1_low[:, 0, :], 0, 1)
+        wa_g1 = staged("wa_g1")
+        cast_on_gpsimd(wa_raw[1][:], wa_g1[:])
         quantize(wa_c[1][:], wa_s[1][:], wa_g1[:])
         a1 = project_a(1)
 
-        warm = bank(7, [P, H], "warm")
+        warm = bank(3, [P, H], "warm")
         for t in range(WARMUPS):
-            project_b(warm, t)
-
-        bq1_high = keep.tile([P, PACK - 1, HALF], BF16, name="bq1_high", tag="late", align_bytes=64)
-        for t in range(1, PACK):
-            gather_b(bq1_high[:, t - 1, :], t, 1)
+            project_b(warm[:], t, slice(0, H))
 
         zp01 = sb([P, PACK, HALF], BF16, "zp01")
         zp23 = sb([P, PACK, HALF], BF16, "zp23")
-        larger(zp01[:], a0[:], bq0[:])
+        for u in range(2):
+            larger(zp01[:, 2 * u : 2 * u + 2, :], a0[:, 2 * u : 2 * u + 2, :], bq0[u])
+        zu0 = interleave(0, zp01[:, :, 0:CHUNK], nc.scalar.copy)
         zu1 = interleave(1, zp01[:, :, CHUNK:HALF], nc.scalar.copy)
-        larger(zp23[:, 0:1, :], a1[:, 0:1, :], bq1_low[:])
-        zu0 = interleave(0, zp01[:, :, 0:CHUNK], nc.vector.tensor_copy)
+        bq1_high = keep.tile([P, PACK - 1, HALF], BF16, name="bq1_high", tag="bq0_0", align_bytes=64)
+        for t in range(1, PACK):
+            gather_b(bq1_high[:, t - 1, :], t, 1)
+        larger(zp23[:, 0:1, :], a1[:, 0:1, :], bq1_low)
         larger(zp23[:, 1:PACK, :], a1[:, 1:PACK, :], bq1_high[:])
-        z0 = signed(0, zu0)
         zu2 = interleave(2, zp23[:, :, 0:CHUNK], nc.scalar.copy)
         zu3 = interleave(3, zp23[:, :, CHUNK:HALF], nc.scalar.copy)
-        y0 = mix_chunk(0, *quantize_z(0, z0))
+        z0 = signed(0, zu0)
         z1 = signed(1, zu1)
-        z2 = signed(2, zu2)
+        y0 = mix_chunk(0, *quantize_z(0, z0))
         y1 = mix_chunk(1, *quantize_z(1, z1))
+        z2 = signed(2, zu2)
         z3 = signed(3, zu3)
         y2 = mix_chunk(2, *quantize_z(2, z2))
         y3 = mix_chunk(3, *quantize_z(3, z3))

@@ -47,9 +47,7 @@ def tile_picked_tokmax_none_po_kernel(
         w1w = sb([P, 2 * N], U8, "w1w")
         w1s = sb([P, N], U8, "w1s")
         g = sb([P, PACK], F32, "g")
-        wb_half = sb([P, PACK, HALF], F32, "wb_half")
-        wb_third = sb([P, PACK, CHUNK], F32, "wb_third")
-        wb_last = keep.tile([P, PACK, CHUNK], F32, name="wb_last", tag="wb_last", align_bytes=64)
+        wb_raw = [keep.tile([P, PACK, HALF], F32, name="wb_raw%d" % h, tag="wb_raw%d" % h, align_bytes=64) for h in range(2)]
         wa_raw = [keep.tile([P, PACK, HALF], F32, name="wa_raw%d" % h, tag="wa_raw%d" % h, align_bytes=64) for h in range(2)]
 
         nc.vector.memset(xs[:].bitcast(I32), 0)
@@ -69,12 +67,11 @@ def tile_picked_tokmax_none_po_kernel(
         nc.sync.dma_start(out=xw[:], in_=x_words[0].rearrange("p n t -> p (n t)").bitcast(I32))
         load_scale_rows(w1s, w1_scales, (nc.sync,) * 4)
         nc.sync.dma_start(out=g[:], in_=gt.rearrange("(p t) o -> p (t o)", t=PACK))
-        nc.sync.dma_start(out=wb_half[:], in_=wb_v[:, :, 0:HALF])
-        nc.sync.dma_start(out=wb_third[:], in_=wb_v[:, :, HALF : HALF + CHUNK])
-        nc.sync.dma_start(out=wb_last[:], in_=wb_v[:, :, HALF + CHUNK : H])
-        nc.sync.dma_start(fl_t[:], fl)
         for h in range(2):
-            nc.sync.dma_start(out=wa_raw[h][:], in_=wa_v[:, :, h * HALF : (h + 1) * HALF])
+            nc.sync.dma_start(out=wb_raw[h][:], in_=wb_v[:, :, h * HALF : (h + 1) * HALF])
+        nc.sync.dma_start(out=wa_raw[0][:], in_=wa_v[:, :, 0:HALF])
+        nc.sync.dma_start(fl_t[:], fl)
+        nc.sync.dma_start(out=wa_raw[1][:], in_=wa_v[:, :, HALF:H])
 
         def cast(copy, raw, grouped):
             copy(
@@ -131,13 +128,12 @@ def tile_picked_tokmax_none_po_kernel(
         wa_c = [sb([P, HALF], U32, "wa_c%d" % h) for h in range(2)]
         wa_s = [sb([P, HALF], U8, "wa_s%d" % h) for h in range(2)]
         quarter = CHUNK * PACK
-        cast(nc.scalar.copy, wb_half[:, :, 0:CHUNK], wb_g[0][:, 0:quarter])
-        cast_on_gpsimd(wb_half[:, :, CHUNK:HALF], wb_g[0][:, quarter : 2 * quarter])
-        cast(nc.scalar.copy, wb_third[:], wb_g[1][:, 0:quarter])
-        cast(nc.scalar.copy, wb_last[:], wb_g[1][:, quarter : 2 * quarter])
+        cast(nc.scalar.copy, wb_raw[0][:], wb_g[0][:])
+        cast(nc.scalar.copy, wb_raw[1][:, :, 0:CHUNK], wb_g[1][:, 0:quarter])
+        cast(nc.vector.tensor_copy, wb_raw[1][:, :, CHUNK:HALF], wb_g[1][:, quarter : 2 * quarter])
         for h in range(2):
             quantize(wb_c[:, h * HALF : (h + 1) * HALF], wb_s[:, h * HALF : (h + 1) * HALF], wb_g[h][:])
-        xa_w = gather_words(offs_t, "xa_w", "wb_last")
+        xa_w = gather_words(offs_t, "xa_w", "wb_raw1")
 
         def rows(t):
             return slice(t * P, (t + 1) * P)
@@ -150,16 +146,16 @@ def tile_picked_tokmax_none_po_kernel(
 
         b_sb = [sb([P, H], F32, "b_sb%d" % t) for t in range(PACK)]
 
-        def half_of_b(t, h):
-            cols = slice(h * HALF, (h + 1) * HALF)
-            acc = bank(PACK * h + t, [P, HALF], "b_acc%d_%d" % (t, h))
+        def part_of_b(t, cols, which):
+            acc = bank(which, [P, cols.stop - cols.start], "b_acc%d" % which)
             project_b(acc[:], t, cols)
             nc.scalar.activation(out=b_sb[t][:, cols], in_=acc[:], func=ACT.Copy, scale=g_abs[:, t : t + 1])
 
-        for pair in range(2):
-            for h in range(2):
-                for t in (2 * pair, 2 * pair + 1):
-                    half_of_b(t, h)
+        for h in range(2):
+            for t in range(2):
+                part_of_b(t, slice(h * HALF, (h + 1) * HALF), 4 + 2 * h + t)
+        for t in range(2, PACK):
+            part_of_b(t, slice(0, H), t)
 
         def project_a(h):
             a_h = sb([P, PACK, HALF], BF16, "a_sb%d" % h)
@@ -238,21 +234,21 @@ def tile_picked_tokmax_none_po_kernel(
             cols = slice(c * CHUNK, (c + 1) * CHUNK)
             quantize(y_c[:, cols], y_s[:, cols], yg[:])
 
-        bq0 = [keep.tile([P, 2, HALF], BF16, name="bq0_0", tag="bq0_0", align_bytes=64)[:], None]
-        for t in range(2):
-            gather_b(bq0[0][:, t, :], t, 0)
+        wa_g1 = sb([P, HALF * PACK], BF16, "wa_g1")
+        cast(nc.scalar.copy, wa_raw[1][:], wa_g1[:])
+
+        def gathered(name, tag, pieces):
+            tile = keep.tile([P, len(pieces), HALF], BF16, name=name, tag=tag, align_bytes=64)
+            for i, (t, h) in enumerate(pieces):
+                gather_b(tile[:, i, :], t, h)
+            return tile
+
+        bq_first = gathered("bq_first", "bq_first", [(0, 0), (1, 0), (2, 0)])
         wa_g0 = staged("wa_g0")
         cast_on_gpsimd(wa_raw[0][:], wa_g0[:])
         quantize(wa_c[0][:], wa_s[0][:], wa_g0[:])
         a0 = project_a(0)
-        held = keep.tile([P, 3, HALF], BF16, name="held", tag="wa_raw0", align_bytes=64)
-        bq0[1] = held[:, 0:2, :]
-        for t in range(2, PACK):
-            gather_b(bq0[1][:, t - 2, :], t, 0)
-        bq1_low = held[:, 2:3, :]
-        gather_b(bq1_low[:, 0, :], 0, 1)
-        wa_g1 = staged("wa_g1")
-        cast_on_gpsimd(wa_raw[1][:], wa_g1[:])
+        bq_second = gathered("bq_second", "wa_raw0", [(3, 0), (0, 1)])
         quantize(wa_c[1][:], wa_s[1][:], wa_g1[:])
         a1 = project_a(1)
 
@@ -262,15 +258,15 @@ def tile_picked_tokmax_none_po_kernel(
 
         zp01 = sb([P, PACK, HALF], BF16, "zp01")
         zp23 = sb([P, PACK, HALF], BF16, "zp23")
-        for u in range(2):
-            larger(zp01[:, 2 * u : 2 * u + 2, :], a0[:, 2 * u : 2 * u + 2, :], bq0[u])
+        bq_third = gathered("bq_third", "wa_raw1", [(1, 1), (2, 1)])
+        larger(zp01[:, 0:3, :], a0[:, 0:3, :], bq_first[:])
+        larger(zp01[:, 3:4, :], a0[:, 3:4, :], bq_second[:, 0:1, :])
         zu0 = interleave(0, zp01[:, :, 0:CHUNK], nc.scalar.copy)
         zu1 = interleave(1, zp01[:, :, CHUNK:HALF], nc.scalar.copy)
-        bq1_high = keep.tile([P, PACK - 1, HALF], BF16, name="bq1_high", tag="bq0_0", align_bytes=64)
-        for t in range(1, PACK):
-            gather_b(bq1_high[:, t - 1, :], t, 1)
-        larger(zp23[:, 0:1, :], a1[:, 0:1, :], bq1_low)
-        larger(zp23[:, 1:PACK, :], a1[:, 1:PACK, :], bq1_high[:])
+        bq_last = gathered("bq_last", "bq_first", [(3, 1)])
+        larger(zp23[:, 0:1, :], a1[:, 0:1, :], bq_second[:, 1:2, :])
+        larger(zp23[:, 1:3, :], a1[:, 1:3, :], bq_third[:])
+        larger(zp23[:, 3:4, :], a1[:, 3:4, :], bq_last[:])
         zu2 = interleave(2, zp23[:, :, 0:CHUNK], nc.scalar.copy)
         zu3 = interleave(3, zp23[:, :, CHUNK:HALF], nc.scalar.copy)
         z0 = signed(0, zu0)

@@ -22,6 +22,7 @@ HALF = H // 2
 CHUNK = 128
 CHUNKS = H // CHUNK
 LINE = 4
+SLOW = 192
 WARMUPS = 2
 
 
@@ -154,6 +155,8 @@ def tile_picked_tokmax_none_po_kernel(
         for h in range(2):
             for t in range(2):
                 part_of_b(t, slice(h * HALF, (h + 1) * HALF), 4 + 2 * h + t)
+        wa_g0 = staged("wa_g0")
+        cast(nc.scalar.copy, wa_raw[0][:, :, SLOW:HALF], wa_g0[:, SLOW * PACK : HALF * PACK])
         for t in range(2, PACK):
             part_of_b(t, slice(0, H), t)
 
@@ -244,8 +247,7 @@ def tile_picked_tokmax_none_po_kernel(
             return tile
 
         bq_first = gathered("bq_first", "bq_first", [(0, 0), (1, 0), (2, 0)])
-        wa_g0 = staged("wa_g0")
-        cast_on_gpsimd(wa_raw[0][:], wa_g0[:])
+        cast_on_gpsimd(wa_raw[0][:, :, 0:SLOW], wa_g0[:, 0 : SLOW * PACK])
         quantize(wa_c[0][:], wa_s[0][:], wa_g0[:])
         a0 = project_a(0)
         bq_second = gathered("bq_second", "wa_raw0", [(3, 0), (0, 1)])

@@ -20,10 +20,7 @@ P = 128
 PACK = 4
 HALF = H // 2
 CHUNK = 128
-CHUNKS = H // CHUNK
 LINE = 4
-SLOW = 192
-WARMUPS = 2
 
 
 def tile_picked_tokmax_none_po_kernel(
@@ -48,8 +45,8 @@ def tile_picked_tokmax_none_po_kernel(
         w1w = sb([P, 2 * N], U8, "w1w")
         w1s = sb([P, N], U8, "w1s")
         g = sb([P, PACK], F32, "g")
-        wb_raw = [keep.tile([P, PACK, HALF], F32, name="wb_raw%d" % h, tag="wb_raw%d" % h, align_bytes=64) for h in range(2)]
-        wa_raw = [keep.tile([P, PACK, HALF], F32, name="wa_raw%d" % h, tag="wa_raw%d" % h, align_bytes=64) for h in range(2)]
+        wb_raw = [sb([P, PACK, HALF], F32, "wb_raw%d" % h) for h in range(2)]
+        wa_raw = [sb([P, PACK, HALF], F32, "wa_raw%d" % h) for h in range(2)]
 
         nc.vector.memset(xs[:].bitcast(I32), 0)
         nc.vector.memset(w1s[:].bitcast(I32), 0)
@@ -66,34 +63,29 @@ def tile_picked_tokmax_none_po_kernel(
         nc.sync.dma_start(offs_t[:], offs)
         load_scale_rows(xs, x_scales, (nc.sync, nc.sync, nc.scalar, nc.scalar))
         nc.sync.dma_start(out=xw[:], in_=x_words[0].rearrange("p n t -> p (n t)").bitcast(I32))
-        load_scale_rows(w1s, w1_scales, (nc.sync,) * 4)
-        nc.sync.dma_start(out=g[:], in_=gt.rearrange("(p t) o -> p (t o)", t=PACK))
         for h in range(2):
             nc.sync.dma_start(out=wb_raw[h][:], in_=wb_v[:, :, h * HALF : (h + 1) * HALF])
         nc.sync.dma_start(out=wa_raw[0][:], in_=wa_v[:, :, 0:HALF])
         nc.sync.dma_start(fl_t[:], fl)
         nc.sync.dma_start(out=wa_raw[1][:], in_=wa_v[:, :, HALF:H])
+        nc.sync.dma_start(out=g[:], in_=gt.rearrange("(p t) o -> p (t o)", t=PACK))
+        load_scale_rows(w1s, w1_scales, (nc.sync,) * 4)
 
-        def cast(copy, raw, grouped):
-            copy(
-                out=grouped.rearrange("p (c i j) -> p c j i", i=LINE, j=PACK),
-                in_=raw.rearrange("p j (c i) -> p c j i", i=LINE),
-            )
+        def walk(ap):
+            return ap.rearrange("p t (c i) -> p c t i", i=LINE)
+
+        def woven(ap):
+            return ap.rearrange("p (c i t) -> p c t i", i=LINE, t=PACK)
+
+        def cast(copy, planes, grouped):
+            copy(out=woven(grouped), in_=walk(planes))
 
         def quantize(codes, scales, values):
             nc.vector.quantize_mx(out=codes.bitcast(FP8X4), scales=scales, in_=values)
 
-        def deal_bytes(plain, name):
-            dealt = sb([P, plain.shape[1]], U8, name)
-            nc.vector.tensor_copy(
-                out=dealt[:].rearrange("p (l t m) -> p l t m", t=PACK, m=P),
-                in_=plain[:].rearrange("p (l m t) -> p l t m", t=PACK, m=P),
-            )
-            return dealt
-
-        def gather_words(lst, name, tag):
-            dealt = keep.tile([P, S], U32, name=name, tag=tag, align_bytes=64)
-            nc.vector.tensor_copy(dealt[:].rearrange("p (t m) -> p m t", t=PACK), xw[:].bitcast(U32).indirect(lst[:]))
+        def pick(table, lst, dtype, name):
+            dealt = sb([P, S], dtype, name)
+            nc.vector.tensor_copy(dealt[:].rearrange("p (t m) -> p m t", t=PACK), table.indirect(lst[:]))
             return dealt
 
         w1w_d = sb([P, 2 * N], U8, "w1w_d")
@@ -101,194 +93,141 @@ def tile_picked_tokmax_none_po_kernel(
             out=w1w_d[:].rearrange("p (t m b) -> p t m b", t=PACK, b=2),
             in_=w1w[:].rearrange("p (m t b) -> p t m b", t=PACK, b=2),
         )
-        picked_s = sb([P, 2 * S], U8, "picked_s")
-        nc.vector.tensor_copy(picked_s[:, 0:S], xs[:].indirect(two_t[:]))
-        nc.vector.tensor_copy(picked_s[:, S : 2 * S], xs[:].indirect(offs_t[:]))
-        x_s = deal_bytes(picked_s, "x_s")
-        xb_s, xa_s = x_s[:, 0:S], x_s[:, S : 2 * S]
-        xb_w = gather_words(two_t, "xb_w", "xb_w")
-        w1s_d = deal_bytes(w1s, "w1s_d")
-
-        g_abs = sb([P, PACK], F32, "g_abs")
-        g_sign = sb([P, PACK], BF16, "g_sign")
-        nc.scalar.activation(out=g_abs[:], in_=g[:], func=ACT.Abs)
-        nc.scalar.activation(out=g_sign[:], in_=g[:], func=ACT.Sign)
-
-        def cast_on_gpsimd(raw, grouped):
-            nc.gpsimd.tensor_scalar(
-                out=grouped.rearrange("p (c j) -> p c j", j=PACK), in0=raw.rearrange("p j c -> p c j"),
-                scalar1=1.0, scalar2=0.0, op0=ALU.mult, op1=ALU.add,
-            )
+        xb_s = pick(xs[:], two_t, U8, "xb_s")
+        xa_s = pick(xs[:], offs_t, U8, "xa_s")
+        xb_w = pick(xw[:].bitcast(U32), two_t, U32, "xb_w")
+        xa_w = pick(xw[:].bitcast(U32), offs_t, U32, "xa_w")
 
         def staged(name):
             return keep.tile([P, HALF * PACK], BF16, name=name, tag="staged", align_bytes=64)
 
         wb_g = [sb([P, HALF * PACK], BF16, "wb_g0"), staged("wb_g1")]
-        wb_c = sb([P, H], U32, "wb_c")
-        wb_s = sb([P, H], U8, "wb_s")
+        wb_c = [sb([P, HALF], U32, "wb_c%d" % h) for h in range(2)]
+        wb_s = [sb([P, HALF], U8, "wb_s%d" % h) for h in range(2)]
         wa_c = [sb([P, HALF], U32, "wa_c%d" % h) for h in range(2)]
         wa_s = [sb([P, HALF], U8, "wa_s%d" % h) for h in range(2)]
-        quarter = CHUNK * PACK
         cast(nc.scalar.copy, wb_raw[0][:], wb_g[0][:])
-        cast(nc.scalar.copy, wb_raw[1][:, :, 0:CHUNK], wb_g[1][:, 0:quarter])
-        cast(nc.vector.tensor_copy, wb_raw[1][:, :, CHUNK:HALF], wb_g[1][:, quarter : 2 * quarter])
-        for h in range(2):
-            quantize(wb_c[:, h * HALF : (h + 1) * HALF], wb_s[:, h * HALF : (h + 1) * HALF], wb_g[h][:])
-        xa_w = gather_words(offs_t, "xa_w", "wb_raw1")
+        cast(nc.scalar.copy, wb_raw[1][:], wb_g[1][:])
 
         def rows(t):
             return slice(t * P, (t + 1) * P)
 
-        def project_b(acc, t, cols):
+        def project(acc, x_w, x_s, t, w_c, w_s):
             nc.tensor.matmul_mx(
-                out=acc, lhsT=xb_w[:, rows(t)].bitcast(FP8X4), lhsT_scale=xb_s[:, rows(t)],
-                rhs=wb_c[:, cols].bitcast(FP8X4), rhs_scale=wb_s[:, cols], start=True, stop=True,
+                out=acc, lhsT=x_w[:, rows(t)].bitcast(FP8X4), lhsT_scale=x_s[:, rows(t)],
+                rhs=w_c.bitcast(FP8X4), rhs_scale=w_s, start=True, stop=True,
             )
 
-        b_sb = [sb([P, H], F32, "b_sb%d" % t) for t in range(PACK)]
-
-        def part_of_b(t, cols, which):
-            acc = bank(which, [P, cols.stop - cols.start], "b_acc%d" % which)
-            project_b(acc[:], t, cols)
-            nc.scalar.activation(out=b_sb[t][:, cols], in_=acc[:], func=ACT.Copy, scale=g_abs[:, t : t + 1])
-
+        b_acc = [bank(t, [P, 2, HALF], "b_acc%d" % t) for t in range(PACK)]
         for h in range(2):
-            for t in range(2):
-                part_of_b(t, slice(h * HALF, (h + 1) * HALF), 4 + 2 * h + t)
-        wa_g0 = staged("wa_g0")
-        cast(nc.scalar.copy, wa_raw[0][:, :, SLOW:HALF], wa_g0[:, SLOW * PACK : HALF * PACK])
-        for t in range(2, PACK):
-            part_of_b(t, slice(0, H), t)
+            quantize(wb_c[h][:], wb_s[h][:], wb_g[h][:])
+            for t in range(PACK):
+                project(b_acc[t][:, h, :], xb_w, xb_s, t, wb_c[h][:], wb_s[h][:])
+
+        b_sb = [sb([P, H], F32, "b_sb%d" % t) for t in range(PACK)]
+        for t in range(PACK):
+            copy = nc.vector.tensor_copy if t == 1 else nc.scalar.copy
+            copy(out=b_sb[t][:], in_=b_acc[t][:].rearrange("p h c -> p (h c)"))
 
         def project_a(h):
-            a_h = sb([P, PACK, HALF], BF16, "a_sb%d" % h)
+            wa_g = staged("wa_g%d" % h)
+            cast(nc.vector.tensor_copy, wa_raw[h][:], wa_g[:])
+            quantize(wa_c[h][:], wa_s[h][:], wa_g[:])
+            accs = [bank(4 + 2 * h + u, [P, 2, HALF], "a_acc%d_%d" % (h, u)) for u in range(2)]
+            for t in range(PACK):
+                project(accs[t // 2][:, t % 2, :], xa_w, xa_s, t, wa_c[h][:], wa_s[h][:])
+            return accs
+
+        def gather_b(h, on_vector):
+            bq = [keep.tile([P, 2, HALF], F32, name="bq%d_%d" % (h, u), tag="bq%d" % u, align_bytes=64) for u in range(2)]
+            for t in range(PACK):
+                picked = b_sb[t][:].indirect(fl_t[:, h * HALF // 16 : (h + 1) * HALF // 16])
+                if t in on_vector:
+                    nc.vector.tensor_copy(bq[t // 2][:, t % 2, :], picked)
+                else:
+                    nc.scalar.activation(out=bq[t // 2][:, t % 2, :], in_=picked, func=ACT.Copy)
+            return bq
+
+        def larger(h, accs, bq):
+            m = keep.tile([P, PACK, HALF], F32, name="m%d" % h, tag="m", align_bytes=64)
             for u in range(2):
-                acc = bank(2 * h + u, [P, 2, HALF], "a_acc%d_%d" % (h, u))
-                for v in range(2):
-                    t = 2 * u + v
-                    nc.tensor.matmul_mx(
-                        out=acc[:, v, :], lhsT=xa_w[:, rows(t)].bitcast(FP8X4), lhsT_scale=xa_s[:, rows(t)],
-                        rhs=wa_c[h][:].bitcast(FP8X4), rhs_scale=wa_s[h][:], start=True, stop=True,
-                    )
-                for v in range(2):
-                    t = 2 * u + v
-                    nc.scalar.activation(out=a_h[:, t, :], in_=acc[:, v, :], func=ACT.Copy, scale=g_abs[:, t : t + 1])
-            return a_h
+                nc.vector.tensor_tensor(out=m[:, 2 * u : 2 * u + 2, :], in0=accs[u][:], in1=bq[u][:], op=ALU.max)
+            return m
 
-        def gather_b(bq_ap, t, h):
-            nc.vector.tensor_copy(bq_ap, b_sb[t][:].indirect(fl_t[:, h * HALF // 16 : (h + 1) * HALF // 16]))
-
-        def walk(ap):
-            return ap.rearrange("p t (c i) -> p c t i", i=LINE)
-
-        def larger(zp_ap, a_ap, bq_ap):
-            nc.vector.tensor_tensor(out=zp_ap, in0=a_ap, in1=bq_ap, op=ALU.max)
-
-        def interleave(c, zp, copy):
-            zu = sb([P, CHUNK * PACK], BF16, "zu%d" % c)
-            copy(out=zu[:].rearrange("p (c i t) -> p c t i", i=LINE, t=PACK), in_=walk(zp))
-            return zu
-
-        def signed(c, zu):
-            z = sb([P, CHUNK * PACK], BF16, "z%d" % c)
+        def weigh(name, m_ap):
+            width = m_ap.shape[2]
+            z = sb([P, width * PACK], BF16, name)
             nc.vector.tensor_tensor(
-                out=z[:].rearrange("p (n t) -> p n t", t=PACK),
-                in0=zu[:].rearrange("p (n t) -> p n t", t=PACK),
-                in1=g_sign[:].unsqueeze(1).to_broadcast([P, CHUNK, PACK]),
-                op=ALU.mult,
+                out=woven(z[:]), in0=walk(m_ap),
+                in1=g[:].unsqueeze(1).unsqueeze(3).to_broadcast([P, width // LINE, PACK, LINE]), op=ALU.mult,
             )
             return z
 
-        def quantize_z(c, z):
-            z_c = sb([P, CHUNK], U32, "z_c%d" % c)
-            z_s = sb([P, CHUNK], U8, "z_s%d" % c)
+        def quantize_z(name, z):
+            width = z.shape[1] // PACK
+            z_c = sb([P, width], U32, name + "_c")
+            z_s = sb([P, width], U8, name + "_s")
             quantize(z_c[:], z_s[:], z[:])
             return z_c, z_s
-
-        def mix(acc_ap, t, z_c, z_s):
-            nc.tensor.matmul_mx(
-                out=acc_ap, lhsT=w1w_d[:, 2 * P * t : 2 * P * (t + 1)].bitcast(FP4X4), lhsT_scale=w1s_d[:, rows(t)],
-                rhs=z_c[:].bitcast(FP8X4), rhs_scale=z_s[:], start=True, stop=True,
-            )
 
         out_v = out_0.rearrange("(p t) j -> p t j", t=PACK)
         words_v = out_1[0].rearrange("p n r -> p (n r)").bitcast(I32)
         y_s = sb([P, H], U8, "y_s")
         y_c = sb([P, H], I32, "y_c")
 
-        def mix_chunk(c, z_c, z_s):
+        def mix(c, z_c, z_s):
+            acc = bank(c, [P, PACK, CHUNK], "y_acc%d" % c)
+            for t in range(PACK):
+                nc.tensor.matmul_mx(
+                    out=acc[:, t, :], lhsT=w1w_d[:, 2 * P * t : 2 * P * (t + 1)].bitcast(FP4X4), lhsT_scale=w1s_d[:, rows(t)],
+                    rhs=z_c.bitcast(FP8X4), rhs_scale=z_s, start=True, stop=True,
+                )
             y = sb([P, PACK, CHUNK], F32, "y%d" % c)
-            parts = 2 if c == CHUNKS - 1 else 1
-            per = PACK // parts
-            for u in range(parts):
-                acc = bank(3 + (1 + c + u) % 5, [P, per, CHUNK], "y_acc%d_%d" % (c, u))
-                for v in range(per):
-                    mix(acc[:, v, :], u * per + v, z_c, z_s)
-                nc.scalar.copy(out=y[:, u * per : (u + 1) * per, :], in_=acc[:])
+            nc.scalar.copy(out=y[:], in_=acc[:])
             nc.sync.dma_start(out=out_v[:, :, c * CHUNK : (c + 1) * CHUNK], in_=y[:])
             return y
 
-        def round_y(c, y):
-            yg = sb([P, CHUNK * PACK], BF16, "yg%d" % c)
-            nc.vector.tensor_copy(out=yg[:].rearrange("p (c i t) -> p c t i", i=LINE, t=PACK), in_=walk(y[:]))
-            return yg
+        yg = sb([P, H * PACK], BF16, "yg")
 
-        def quantize_y(c, yg):
-            cols = slice(c * CHUNK, (c + 1) * CHUNK)
-            quantize(y_c[:, cols], y_s[:, cols], yg[:])
+        def round_y(c, y, copy):
+            cast(copy, y[:], yg[:, c * CHUNK * PACK : (c + 1) * CHUNK * PACK])
 
-        wa_g1 = sb([P, HALF * PACK], BF16, "wa_g1")
-        cast(nc.scalar.copy, wa_raw[1][:], wa_g1[:])
+        def quantize_y(first, last):
+            cols = slice(first * CHUNK, last * CHUNK)
+            quantize(y_c[:, cols], y_s[:, cols], yg[:, first * CHUNK * PACK : last * CHUNK * PACK])
 
-        def gathered(name, tag, pieces):
-            tile = keep.tile([P, len(pieces), HALF], BF16, name=name, tag=tag, align_bytes=64)
-            for i, (t, h) in enumerate(pieces):
-                gather_b(tile[:, i, :], t, h)
-            return tile
-
-        bq_first = gathered("bq_first", "bq_first", [(0, 0), (1, 0), (2, 0)])
-        cast_on_gpsimd(wa_raw[0][:, :, 0:SLOW], wa_g0[:, 0 : SLOW * PACK])
-        quantize(wa_c[0][:], wa_s[0][:], wa_g0[:])
         a0 = project_a(0)
-        bq_second = gathered("bq_second", "wa_raw0", [(3, 0), (0, 1)])
-        quantize(wa_c[1][:], wa_s[1][:], wa_g1[:])
         a1 = project_a(1)
-
-        warm = bank(3, [P, H], "warm")
-        for t in range(WARMUPS):
-            project_b(warm[:], t, slice(0, H))
-
-        zp01 = sb([P, PACK, HALF], BF16, "zp01")
-        zp23 = sb([P, PACK, HALF], BF16, "zp23")
-        bq_third = gathered("bq_third", "wa_raw1", [(1, 1), (2, 1)])
-        larger(zp01[:, 0:3, :], a0[:, 0:3, :], bq_first[:])
-        larger(zp01[:, 3:4, :], a0[:, 3:4, :], bq_second[:, 0:1, :])
-        zu0 = interleave(0, zp01[:, :, 0:CHUNK], nc.scalar.copy)
-        zu1 = interleave(1, zp01[:, :, CHUNK:HALF], nc.scalar.copy)
-        bq_last = gathered("bq_last", "bq_first", [(3, 1)])
-        larger(zp23[:, 0:1, :], a1[:, 0:1, :], bq_second[:, 1:2, :])
-        larger(zp23[:, 1:3, :], a1[:, 1:3, :], bq_third[:])
-        larger(zp23[:, 3:4, :], a1[:, 3:4, :], bq_last[:])
-        zu2 = interleave(2, zp23[:, :, 0:CHUNK], nc.scalar.copy)
-        zu3 = interleave(3, zp23[:, :, CHUNK:HALF], nc.scalar.copy)
-        z0 = signed(0, zu0)
-        z1 = signed(1, zu1)
-        y0 = mix_chunk(0, *quantize_z(0, z0))
-        y1 = mix_chunk(1, *quantize_z(1, z1))
-        z2 = signed(2, zu2)
-        z3 = signed(3, zu3)
-        y2 = mix_chunk(2, *quantize_z(2, z2))
-        y3 = mix_chunk(3, *quantize_z(3, z3))
-        yg0 = round_y(0, y0)
-        yg1 = round_y(1, y1)
-        quantize_y(0, yg0)
-        yg2 = round_y(2, y2)
-        quantize_y(1, yg1)
-        quantize_y(2, yg2)
+        bq0 = gather_b(0, (3,))
+        w1s_d = sb([P, N], U8, "w1s_d")
+        nc.vector.tensor_copy(
+            out=w1s_d[:].rearrange("p (t m) -> p t m", t=PACK), in_=w1s[:].rearrange("p (m t) -> p t m", t=PACK)
+        )
+        m0 = larger(0, a0, bq0)
+        bq1 = gather_b(1, ())
+        z0 = weigh("z0", m0[:, :, 0:CHUNK])
+        z1 = weigh("z1", m0[:, :, CHUNK:HALF])
+        zq0 = quantize_z("zq0", z0)
+        zq1 = quantize_z("zq1", z1)
+        y0 = mix(0, zq0[0][:], zq0[1][:])
+        y1 = mix(1, zq1[0][:], zq1[1][:])
+        round_y(0, y0, nc.scalar.copy)
+        round_y(1, y1, nc.scalar.copy)
+        m1 = larger(1, a1, bq1)
+        z2 = weigh("z2", m1[:, :, 0:CHUNK])
+        z3 = weigh("z3", m1[:, :, CHUNK:HALF])
+        zq2 = quantize_z("zq2", z2)
+        zq3 = quantize_z("zq3", z3)
+        y2 = mix(2, zq2[0][:], zq2[1][:])
+        y3 = mix(3, zq3[0][:], zq3[1][:])
+        quantize_y(0, 2)
+        round_y(2, y2, nc.vector.tensor_copy)
+        quantize_y(2, 3)
 
         last = H - CHUNK
         nc.sync.dma_start(out=words_v[:, 0:last], in_=y_c[:, 0:last])
-        quantize_y(3, round_y(3, y3))
+        round_y(3, y3, nc.vector.tensor_copy)
+        quantize_y(3, 4)
         nc.sync.dma_start(out=words_v[:, last:H], in_=y_c[:, last:H])
         for q in range(4):
             eng = nc.scalar if q % 2 else nc.sync

@@ -29,6 +29,7 @@ def tile_picked_tokmax_none_po_kernel(
     nc = tc.nc
     with ExitStack() as ctx:
         keep = ctx.enter_context(tc.tile_pool(name="keep", bufs=1))
+        placed = ctx.enter_context(tc.tile_pool(name="placed", bufs=1))
         psum = ctx.enter_context(tc.psum_pool(name="psum", bufs=1))
 
         def sb(shape, dtype, name):
@@ -62,9 +63,9 @@ def tile_picked_tokmax_none_po_kernel(
         nc.sync.dma_start(two_t[:], two)
         nc.sync.dma_start(offs_t[:], offs)
         load_scale_rows(xs, x_scales, (nc.sync, nc.sync, nc.scalar, nc.scalar))
+        nc.sync.dma_start(out=wb_raw[0][:], in_=wb_v[:, :, 0:HALF])
         nc.sync.dma_start(out=xw[:], in_=x_words[0].rearrange("p n t -> p (n t)").bitcast(I32))
-        for h in range(2):
-            nc.sync.dma_start(out=wb_raw[h][:], in_=wb_v[:, :, h * HALF : (h + 1) * HALF])
+        nc.sync.dma_start(out=wb_raw[1][:], in_=wb_v[:, :, HALF:H])
         nc.sync.dma_start(out=wa_raw[0][:], in_=wa_v[:, :, 0:HALF])
         nc.sync.dma_start(fl_t[:], fl)
         nc.sync.dma_start(out=wa_raw[1][:], in_=wa_v[:, :, HALF:H])
@@ -83,8 +84,7 @@ def tile_picked_tokmax_none_po_kernel(
         def quantize(codes, scales, values):
             nc.vector.quantize_mx(out=codes.bitcast(FP8X4), scales=scales, in_=values)
 
-        def pick(table, lst, dtype, name):
-            dealt = sb([P, S], dtype, name)
+        def pick(table, lst, dealt):
             nc.vector.tensor_copy(dealt[:].rearrange("p (t m) -> p m t", t=PACK), table.indirect(lst[:]))
             return dealt
 
@@ -93,18 +93,15 @@ def tile_picked_tokmax_none_po_kernel(
             out=w1w_d[:].rearrange("p (t m b) -> p t m b", t=PACK, b=2),
             in_=w1w[:].rearrange("p (m t b) -> p t m b", t=PACK, b=2),
         )
-        xb_s = pick(xs[:], two_t, U8, "xb_s")
-        xa_s = pick(xs[:], offs_t, U8, "xa_s")
-        xb_w = pick(xw[:].bitcast(U32), two_t, U32, "xb_w")
-        xa_w = pick(xw[:].bitcast(U32), offs_t, U32, "xa_w")
+        xb_s = pick(xs[:], two_t, sb([P, S], U8, "xb_s"))
+        xa_s = pick(xs[:], offs_t, sb([P, S], U8, "xa_s"))
 
         def staged(name):
             return keep.tile([P, HALF * PACK], BF16, name=name, tag="staged", align_bytes=64)
 
-        wb_g = [sb([P, HALF * PACK], BF16, "wb_g0"), staged("wb_g1")]
-        wb_c = [sb([P, HALF], U32, "wb_c%d" % h) for h in range(2)]
-        wb_s = [sb([P, HALF], U8, "wb_s%d" % h) for h in range(2)]
-        wa_c = [sb([P, HALF], U32, "wa_c%d" % h) for h in range(2)]
+        wb_g = [placed.tile([P, HALF * PACK], BF16, name="wb_g0", offset=2 * S, align_bytes=64), staged("wb_g1")]
+        wb_c = sb([P, H], U32, "wb_c")
+        wb_s = sb([P, H], U8, "wb_s")
         wa_s = [sb([P, HALF], U8, "wa_s%d" % h) for h in range(2)]
         cast(nc.scalar.copy, wb_raw[0][:], wb_g[0][:])
         cast(nc.scalar.copy, wb_raw[1][:], wb_g[1][:])
@@ -118,45 +115,62 @@ def tile_picked_tokmax_none_po_kernel(
                 rhs=w_c.bitcast(FP8X4), rhs_scale=w_s, start=True, stop=True,
             )
 
-        b_acc = [bank(t, [P, 2, HALF], "b_acc%d" % t) for t in range(PACK)]
+        b_acc = [bank(t, [P, H], "b_acc%d" % t) for t in range(PACK)]
+        quantize(wb_c[:, 0:HALF], wb_s[:, 0:HALF], wb_g[0][:])
+        xb_w = pick(xw[:].bitcast(U32), two_t, placed.tile([P, S], U32, name="xb_w", offset=0, align_bytes=64))
+        xa_w = pick(xw[:].bitcast(U32), offs_t, placed.tile([P, S], U32, name="xa_w", offset=4 * S, align_bytes=64))
+        quantize(wb_c[:, HALF:H], wb_s[:, HALF:H], wb_g[1][:])
         for h in range(2):
-            quantize(wb_c[h][:], wb_s[h][:], wb_g[h][:])
+            cols = slice(h * HALF, (h + 1) * HALF)
             for t in range(PACK):
-                project(b_acc[t][:, h, :], xb_w, xb_s, t, wb_c[h][:], wb_s[h][:])
+                project(b_acc[t][:, cols], xb_w, xb_s, t, wb_c[:, cols], wb_s[:, cols])
 
         b_sb = [sb([P, H], F32, "b_sb%d" % t) for t in range(PACK)]
-        for t in range(PACK):
-            copy = nc.vector.tensor_copy if t == 1 else nc.scalar.copy
-            copy(out=b_sb[t][:], in_=b_acc[t][:].rearrange("p h c -> p (h c)"))
 
-        def project_a(h):
+        def copy_b(t):
+            copy = nc.vector.tensor_copy if t % 2 else nc.scalar.copy
+            copy(out=b_sb[t][:], in_=b_acc[t][:])
+
+        def cast_wa(h):
             wa_g = staged("wa_g%d" % h)
-            cast(nc.vector.tensor_copy, wa_raw[h][:], wa_g[:])
-            quantize(wa_c[h][:], wa_s[h][:], wa_g[:])
+            nc.gpsimd.tensor_scalar(
+                out=wa_g[:].rearrange("p (c j) -> p c j", j=PACK), in0=wa_raw[h][:].rearrange("p j c -> p c j"),
+                scalar1=1.0, scalar2=0.0, op0=ALU.mult, op1=ALU.add,
+            )
+            return wa_g
+
+        def project_a(h, wa_g, tag):
+            wa_c = keep.tile([P, HALF], U32, name="wa_c%d" % h, tag=tag, align_bytes=64)
+            quantize(wa_c[:], wa_s[h][:], wa_g[:])
             accs = [bank(4 + 2 * h + u, [P, 2, HALF], "a_acc%d_%d" % (h, u)) for u in range(2)]
             for t in range(PACK):
-                project(accs[t // 2][:, t % 2, :], xa_w, xa_s, t, wa_c[h][:], wa_s[h][:])
+                project(accs[t // 2][:, t % 2, :], xa_w, xa_s, t, wa_c[:], wa_s[h][:])
             return accs
 
-        def gather_b(h, on_vector):
-            bq = [keep.tile([P, 2, HALF], F32, name="bq%d_%d" % (h, u), tag="bq%d" % u, align_bytes=64) for u in range(2)]
-            for t in range(PACK):
-                picked = b_sb[t][:].indirect(fl_t[:, h * HALF // 16 : (h + 1) * HALF // 16])
-                if t in on_vector:
-                    nc.vector.tensor_copy(bq[t // 2][:, t % 2, :], picked)
-                else:
-                    nc.scalar.activation(out=bq[t // 2][:, t % 2, :], in_=picked, func=ACT.Copy)
-            return bq
+        def pair_slot(h, u):
+            return keep.tile([P, 2, HALF], F32, name="bq%d_%d" % (h, u), tag="bq%d_%d" % (h, u), align_bytes=64)
 
-        def larger(h, accs, bq):
+        bq = [[pair_slot(0, u) for u in range(2)]]
+
+        def picked_b(h, t):
+            return bq[h][t // 2][:, t % 2, :], b_sb[t][:].indirect(fl_t[:, h * HALF // 16 : (h + 1) * HALF // 16])
+
+        def gather_on_scalar(h, t):
+            out, picked = picked_b(h, t)
+            nc.scalar.activation(out=out, in_=picked, func=ACT.Copy)
+
+        def gather_on_vector(h, t):
+            nc.vector.tensor_copy(*picked_b(h, t))
+
+        def larger(h, accs, picked):
             m = keep.tile([P, PACK, HALF], F32, name="m%d" % h, tag="m", align_bytes=64)
             for u in range(2):
-                nc.vector.tensor_tensor(out=m[:, 2 * u : 2 * u + 2, :], in0=accs[u][:], in1=bq[u][:], op=ALU.max)
+                nc.vector.tensor_tensor(out=m[:, 2 * u : 2 * u + 2, :], in0=accs[u][:], in1=picked[u][:], op=ALU.max)
             return m
 
         def weigh(name, m_ap):
             width = m_ap.shape[2]
-            z = sb([P, width * PACK], BF16, name)
+            z = keep.tile([P, width * PACK], BF16, name=name, tag=name, align_bytes=64)
             nc.vector.tensor_tensor(
                 out=woven(z[:]), in0=walk(m_ap),
                 in1=g[:].unsqueeze(1).unsqueeze(3).to_broadcast([P, width // LINE, PACK, LINE]), op=ALU.mult,
@@ -173,62 +187,68 @@ def tile_picked_tokmax_none_po_kernel(
         out_v = out_0.rearrange("(p t) j -> p t j", t=PACK)
         words_v = out_1[0].rearrange("p n r -> p (n r)").bitcast(I32)
         y_s = sb([P, H], U8, "y_s")
-        y_c = sb([P, H], I32, "y_c")
 
-        def mix(c, z_c, z_s):
-            acc = bank(c, [P, PACK, CHUNK], "y_acc%d" % c)
-            for t in range(PACK):
-                nc.tensor.matmul_mx(
-                    out=acc[:, t, :], lhsT=w1w_d[:, 2 * P * t : 2 * P * (t + 1)].bitcast(FP4X4), lhsT_scale=w1s_d[:, rows(t)],
-                    rhs=z_c.bitcast(FP8X4), rhs_scale=z_s, start=True, stop=True,
-                )
-            y = sb([P, PACK, CHUNK], F32, "y%d" % c)
-            nc.scalar.copy(out=y[:], in_=acc[:])
-            nc.sync.dma_start(out=out_v[:, :, c * CHUNK : (c + 1) * CHUNK], in_=y[:])
+        def mix(first, width, banks, z_c, z_s, copy):
+            y = sb([P, PACK, width], F32, "y%d" % first)
+            per = PACK // len(banks)
+            for u, which in enumerate(banks):
+                acc = bank(which, [P, per, width], "y_acc%d" % which)
+                for v in range(per):
+                    t = u * per + v
+                    nc.tensor.matmul_mx(
+                        out=acc[:, v, :], lhsT=w1w_d[:, 2 * P * t : 2 * P * (t + 1)].bitcast(FP4X4), lhsT_scale=w1s_d[:, rows(t)],
+                        rhs=z_c.bitcast(FP8X4), rhs_scale=z_s, start=True, stop=True,
+                    )
+                copy(out=y[:, u * per : (u + 1) * per, :], in_=acc[:])
+            nc.sync.dma_start(out=out_v[:, :, first : first + width], in_=y[:])
             return y
 
         yg = sb([P, H * PACK], BF16, "yg")
 
-        def round_y(c, y, copy):
-            cast(copy, y[:], yg[:, c * CHUNK * PACK : (c + 1) * CHUNK * PACK])
+        def round_y(first, y, copy):
+            cast(copy, y[:], yg[:, first * PACK : (first + y.shape[2]) * PACK])
 
-        def quantize_y(first, last):
+        def quantize_y(y_c, first, last):
             cols = slice(first * CHUNK, last * CHUNK)
             quantize(y_c[:, cols], y_s[:, cols], yg[:, first * CHUNK * PACK : last * CHUNK * PACK])
 
-        a0 = project_a(0)
-        a1 = project_a(1)
-        bq0 = gather_b(0, (3,))
-        w1s_d = sb([P, N], U8, "w1s_d")
+        wa_g0 = cast_wa(0)
+        for t in range(PACK):
+            copy_b(t)
+        a0 = project_a(0, wa_g0, "wa_c0")
+        wa_g1 = cast_wa(1)
+        for t in range(3):
+            gather_on_scalar(0, t)
+        gather_on_vector(0, 3)
+        m0 = larger(0, a0, bq[0])
+        a1 = project_a(1, wa_g1, "bq0_0")
+        bq.append([pair_slot(1, u) for u in range(2)])
+        for t in range(PACK):
+            gather_on_scalar(1, t)
+        z01 = weigh("z01", m0[:])
+        w1s_d = keep.tile([P, N], U8, name="w1s_d", tag="bq0_1", align_bytes=64)
         nc.vector.tensor_copy(
             out=w1s_d[:].rearrange("p (t m) -> p t m", t=PACK), in_=w1s[:].rearrange("p (m t) -> p t m", t=PACK)
         )
-        m0 = larger(0, a0, bq0)
-        bq1 = gather_b(1, ())
-        z0 = weigh("z0", m0[:, :, 0:CHUNK])
-        z1 = weigh("z1", m0[:, :, CHUNK:HALF])
-        zq0 = quantize_z("zq0", z0)
-        zq1 = quantize_z("zq1", z1)
-        y0 = mix(0, zq0[0][:], zq0[1][:])
-        y1 = mix(1, zq1[0][:], zq1[1][:])
+        zq01 = quantize_z("zq01", z01)
+        y0 = mix(0, CHUNK, (0,), zq01[0][:, 0:CHUNK], zq01[1][:, 0:CHUNK], nc.scalar.copy)
+        y1 = mix(CHUNK, CHUNK, (1,), zq01[0][:, CHUNK:HALF], zq01[1][:, CHUNK:HALF], nc.scalar.copy)
         round_y(0, y0, nc.scalar.copy)
-        round_y(1, y1, nc.scalar.copy)
-        m1 = larger(1, a1, bq1)
+        round_y(CHUNK, y1, nc.scalar.copy)
+        m1 = larger(1, a1, bq[1])
         z2 = weigh("z2", m1[:, :, 0:CHUNK])
         z3 = weigh("z3", m1[:, :, CHUNK:HALF])
         zq2 = quantize_z("zq2", z2)
         zq3 = quantize_z("zq3", z3)
-        y2 = mix(2, zq2[0][:], zq2[1][:])
-        y3 = mix(3, zq3[0][:], zq3[1][:])
-        quantize_y(0, 2)
-        round_y(2, y2, nc.vector.tensor_copy)
-        quantize_y(2, 3)
-
-        last = H - CHUNK
-        nc.sync.dma_start(out=words_v[:, 0:last], in_=y_c[:, 0:last])
-        round_y(3, y3, nc.vector.tensor_copy)
-        quantize_y(3, 4)
-        nc.sync.dma_start(out=words_v[:, last:H], in_=y_c[:, last:H])
+        y2 = mix(HALF, CHUNK, (2,), zq2[0][:], zq2[1][:], nc.scalar.copy)
+        y3 = mix(HALF + CHUNK, CHUNK, (3,), zq3[0][:], zq3[1][:], nc.vector.tensor_copy)
+        y_c = keep.tile([P, H], I32, name="y_c", tag="z3", align_bytes=64)
+        quantize_y(y_c, 0, 2)
+        nc.sync.dma_start(out=words_v[:, 0:HALF], in_=y_c[:, 0:HALF])
+        round_y(HALF, y2, nc.scalar.copy)
+        round_y(HALF + CHUNK, y3, nc.vector.tensor_copy)
+        quantize_y(y_c, 2, 4)
+        nc.sync.dma_start(out=words_v[:, HALF:H], in_=y_c[:, HALF:H])
         for q in range(4):
             eng = nc.scalar if q % 2 else nc.sync
             eng.dma_start(out=out_2[0, 4 * q : 4 * q + 4, :].bitcast(I32), in_=y_s[32 * q : 32 * q + 4, :].bitcast(I32))

@@ -177,18 +177,17 @@ def tile_picked_tokmax_none_po_kernel(
             )
             return z
 
-        def quantize_z(name, z):
-            width = z.shape[1] // PACK
-            z_c = sb([P, width], U32, name + "_c")
-            z_s = sb([P, width], U8, name + "_s")
-            quantize(z_c[:], z_s[:], z[:])
+        def quantize_z(name, z, tag):
+            z_c = keep.tile([P, CHUNK], U32, name=name + "_c", tag=tag, align_bytes=64)
+            z_s = sb([P, CHUNK], U8, name + "_s")
+            quantize(z_c[:], z_s[:], z)
             return z_c, z_s
 
         out_v = out_0.rearrange("(p t) j -> p t j", t=PACK)
         words_v = out_1[0].rearrange("p n r -> p (n r)").bitcast(I32)
         y_s = sb([P, H], U8, "y_s")
 
-        def mix(first, width, banks, z_c, z_s, copy):
+        def mix(first, width, banks, z_c, z_s, copies):
             y = sb([P, PACK, width], F32, "y%d" % first)
             per = PACK // len(banks)
             for u, which in enumerate(banks):
@@ -199,7 +198,7 @@ def tile_picked_tokmax_none_po_kernel(
                         out=acc[:, v, :], lhsT=w1w_d[:, 2 * P * t : 2 * P * (t + 1)].bitcast(FP4X4), lhsT_scale=w1s_d[:, rows(t)],
                         rhs=z_c.bitcast(FP8X4), rhs_scale=z_s, start=True, stop=True,
                     )
-                copy(out=y[:, u * per : (u + 1) * per, :], in_=acc[:])
+                copies[u](out=y[:, u * per : (u + 1) * per, :], in_=acc[:])
             nc.sync.dma_start(out=out_v[:, :, first : first + width], in_=y[:])
             return y
 
@@ -217,9 +216,9 @@ def tile_picked_tokmax_none_po_kernel(
             copy_b(t)
         a0 = project_a(0, wa_g0, "wa_c0")
         wa_g1 = cast_wa(1)
-        for t in range(3):
+        gather_on_vector(0, 1)
+        for t in (0, 2, 3):
             gather_on_scalar(0, t)
-        gather_on_vector(0, 3)
         m0 = larger(0, a0, bq[0])
         a1 = project_a(1, wa_g1, "bq0_0")
         bq.append([pair_slot(1, u) for u in range(2)])
@@ -230,24 +229,27 @@ def tile_picked_tokmax_none_po_kernel(
         nc.vector.tensor_copy(
             out=w1s_d[:].rearrange("p (t m) -> p t m", t=PACK), in_=w1s[:].rearrange("p (m t) -> p t m", t=PACK)
         )
-        zq01 = quantize_z("zq01", z01)
-        y0 = mix(0, CHUNK, (0,), zq01[0][:, 0:CHUNK], zq01[1][:, 0:CHUNK], nc.scalar.copy)
-        y1 = mix(CHUNK, CHUNK, (1,), zq01[0][:, CHUNK:HALF], zq01[1][:, CHUNK:HALF], nc.scalar.copy)
+        zq0 = quantize_z("zq0", z01[:, 0 : CHUNK * PACK], "zq0")
+        y0 = mix(0, CHUNK, (0,), zq0[0][:], zq0[1][:], [nc.scalar.copy])
         round_y(0, y0, nc.scalar.copy)
-        round_y(CHUNK, y1, nc.scalar.copy)
         m1 = larger(1, a1, bq[1])
+        zq1 = quantize_z("zq1", z01[:, CHUNK * PACK : HALF * PACK], "bq1_0")
+        y1 = mix(CHUNK, CHUNK, (1,), zq1[0][:], zq1[1][:], [nc.scalar.copy])
         z2 = weigh("z2", m1[:, :, 0:CHUNK])
         z3 = weigh("z3", m1[:, :, CHUNK:HALF])
-        zq2 = quantize_z("zq2", z2)
-        zq3 = quantize_z("zq3", z3)
-        y2 = mix(HALF, CHUNK, (2,), zq2[0][:], zq2[1][:], nc.scalar.copy)
-        y3 = mix(HALF + CHUNK, CHUNK, (3,), zq3[0][:], zq3[1][:], nc.vector.tensor_copy)
+        zq2 = quantize_z("zq2", z2[:], "zq2")
+        zq3 = quantize_z("zq3", z3[:], "zq3")
+        both = [nc.scalar.copy, nc.vector.tensor_copy]
+        y2 = mix(HALF, CHUNK, (2, 3), zq2[0][:], zq2[1][:], both)
+        y3 = mix(HALF + CHUNK, CHUNK, (4, 5), zq3[0][:], zq3[1][:], [nc.scalar.copy] * 2)
         y_c = keep.tile([P, H], I32, name="y_c", tag="z3", align_bytes=64)
+        round_y(CHUNK, y1, nc.vector.tensor_copy)
         quantize_y(y_c, 0, 2)
         nc.sync.dma_start(out=words_v[:, 0:HALF], in_=y_c[:, 0:HALF])
-        round_y(HALF, y2, nc.scalar.copy)
+        round_y(HALF, y2, nc.vector.tensor_copy)
         round_y(HALF + CHUNK, y3, nc.vector.tensor_copy)
-        quantize_y(y_c, 2, 4)
+        quantize_y(y_c, 2, 3)
+        quantize_y(y_c, 3, 4)
         nc.sync.dma_start(out=words_v[:, HALF:H], in_=y_c[:, HALF:H])
         for q in range(4):
             eng = nc.scalar if q % 2 else nc.sync

@@ -46,7 +46,7 @@ def tile_picked_tokmax_none_po_kernel(
         w1w = sb([P, 2 * N], U8, "w1w")
         w1s = sb([P, N], U8, "w1s")
         g = sb([P, PACK], F32, "g")
-        wb_raw = [sb([P, PACK, HALF], F32, "wb_raw%d" % h) for h in range(2)]
+        wb_raw = [sb([P, PACK, HALF], F32, "wb_raw0"), placed.tile([P, PACK, HALF], F32, name="wb_raw1", offset=10240 + 2048, align_bytes=64)]
         wa_raw = [sb([P, PACK, HALF], F32, "wa_raw%d" % h) for h in range(2)]
 
         nc.vector.memset(xs[:].bitcast(I32), 0)
@@ -96,10 +96,10 @@ def tile_picked_tokmax_none_po_kernel(
         xb_s = pick(xs[:], two_t, sb([P, S], U8, "xb_s"))
         xa_s = pick(xs[:], offs_t, sb([P, S], U8, "xa_s"))
 
-        def staged(name):
-            return keep.tile([P, HALF * PACK], BF16, name=name, tag="staged", align_bytes=64)
+        def staged(name, offset):
+            return placed.tile([P, HALF * PACK], BF16, name=name, offset=offset, align_bytes=64)
 
-        wb_g = [placed.tile([P, HALF * PACK], BF16, name="wb_g0", offset=2 * S, align_bytes=64), staged("wb_g1")]
+        wb_g = [placed.tile([P, HALF * PACK], BF16, name="wb_g0", offset=2 * S, align_bytes=64), staged("wb_g1", 4096 + 2048)]
         wb_c = sb([P, H], U32, "wb_c")
         wb_s = sb([P, H], U8, "wb_s")
         wa_s = [sb([P, HALF], U8, "wa_s%d" % h) for h in range(2)]
@@ -115,7 +115,7 @@ def tile_picked_tokmax_none_po_kernel(
                 rhs=w_c.bitcast(FP8X4), rhs_scale=w_s, start=True, stop=True,
             )
 
-        b_acc = [bank(t, [P, H], "b_acc%d" % t) for t in range(PACK)]
+        b_acc = [[bank(4 * (1 - h) + t, [P, HALF], "b_acc%d_%d" % (h, t)) for t in range(PACK)] for h in range(2)]
         quantize(wb_c[:, 0:HALF], wb_s[:, 0:HALF], wb_g[0][:])
         xb_w = pick(xw[:].bitcast(U32), two_t, placed.tile([P, S], U32, name="xb_w", offset=0, align_bytes=64))
         xa_w = pick(xw[:].bitcast(U32), offs_t, placed.tile([P, S], U32, name="xa_w", offset=4 * S, align_bytes=64))
@@ -123,16 +123,17 @@ def tile_picked_tokmax_none_po_kernel(
         for h in range(2):
             cols = slice(h * HALF, (h + 1) * HALF)
             for t in range(PACK):
-                project(b_acc[t][:, cols], xb_w, xb_s, t, wb_c[:, cols], wb_s[:, cols])
+                project(b_acc[h][t][:], xb_w, xb_s, t, wb_c[:, cols], wb_s[:, cols])
 
-        b_sb = [sb([P, H], F32, "b_sb%d" % t) for t in range(PACK)]
+        b_at = [10240 + 512, 10240 + 2560, 10240 + 4608, 4096 + 256]
+        b_sb = [placed.tile([P, H], F32, name="b_sb%d" % t, offset=b_at[t], align_bytes=64) for t in range(PACK)]
 
-        def copy_b(t):
-            copy = nc.vector.tensor_copy if t % 2 else nc.scalar.copy
-            copy(out=b_sb[t][:], in_=b_acc[t][:])
+        def copy_b(h, t):
+            copy = nc.vector.tensor_copy if t == 3 or (h, t) == (1, 1) else nc.scalar.copy
+            copy(out=b_sb[t][:, h * HALF : (h + 1) * HALF], in_=b_acc[h][t][:])
 
         def cast_wa(h):
-            wa_g = staged("wa_g%d" % h)
+            wa_g = staged("wa_g%d" % h, 4096 + 2304)
             nc.gpsimd.tensor_scalar(
                 out=wa_g[:].rearrange("p (c j) -> p c j", j=PACK), in0=wa_raw[h][:].rearrange("p j c -> p c j"),
                 scalar1=1.0, scalar2=0.0, op0=ALU.mult, op1=ALU.add,
@@ -213,9 +214,12 @@ def tile_picked_tokmax_none_po_kernel(
 
         wa_g0 = cast_wa(0)
         for t in range(PACK):
-            copy_b(t)
+            copy_b(0, t)
+        for t in range(3):
+            copy_b(1, t)
         a0 = project_a(0, wa_g0, "wa_c0")
         wa_g1 = cast_wa(1)
+        copy_b(1, 3)
         gather_on_vector(0, 1)
         for t in (0, 2, 3):
             gather_on_scalar(0, t)

@@ -21,6 +21,8 @@ PACK = 4
 HALF = H // 2
 CHUNK = 128
 LINE = 4
+KIB = 1024
+PAIRS = ((0, 2), (1, 3))
 
 
 def tile_picked_tokmax_none_po_kernel(
@@ -35,6 +37,12 @@ def tile_picked_tokmax_none_po_kernel(
         def sb(shape, dtype, name):
             return keep.tile(shape, dtype, name=name, align_bytes=64)
 
+        def slot(tag, shape, dtype, name):
+            return keep.tile(shape, dtype, name=name, tag=tag, align_bytes=64)
+
+        def at(kib, shape, dtype, name):
+            return placed.tile(shape, dtype, name=name, offset=kib * KIB, align_bytes=64)
+
         def bank(i, shape, name):
             return psum.tile(shape, F32, name=name, tag="bank%d" % i)
 
@@ -46,8 +54,9 @@ def tile_picked_tokmax_none_po_kernel(
         w1w = sb([P, 2 * N], U8, "w1w")
         w1s = sb([P, N], U8, "w1s")
         g = sb([P, PACK], F32, "g")
-        wb_raw = [sb([P, PACK, HALF], F32, "wb_raw0"), placed.tile([P, PACK, HALF], F32, name="wb_raw1", offset=10240 + 2048, align_bytes=64)]
-        wa_raw = [sb([P, PACK, HALF], F32, "wa_raw%d" % h) for h in range(2)]
+
+        wb_raw = [sb([P, PACK, HALF], F32, "wb_raw0"), at(5, [P, PACK, HALF], F32, "wb_raw1")]
+        wa_raw = [at(15, [P, PACK, HALF], F32, "wa_raw0"), sb([P, PACK, HALF], F32, "wa_raw1")]
 
         nc.vector.memset(xs[:].bitcast(I32), 0)
         nc.vector.memset(w1s[:].bitcast(I32), 0)
@@ -88,6 +97,21 @@ def tile_picked_tokmax_none_po_kernel(
             nc.vector.tensor_copy(dealt[:].rearrange("p (t m) -> p m t", t=PACK), table.indirect(lst[:]))
             return dealt
 
+        def rows(t):
+            return slice(t * P, (t + 1) * P)
+
+        def half(h):
+            return slice(h * HALF, (h + 1) * HALF)
+
+        def chunk(c, per=1):
+            return slice(c * CHUNK * per, (c + 1) * CHUNK * per)
+
+        def project(acc, x_w, x_s, t, w_c, w_s):
+            nc.tensor.matmul_mx(
+                out=acc, lhsT=x_w[:, rows(t)].bitcast(FP8X4), lhsT_scale=x_s[:, rows(t)],
+                rhs=w_c.bitcast(FP8X4), rhs_scale=w_s, start=True, stop=True,
+            )
+
         w1w_d = sb([P, 2 * N], U8, "w1w_d")
         nc.vector.tensor_copy(
             out=w1w_d[:].rearrange("p (t m b) -> p t m b", t=PACK, b=2),
@@ -96,165 +120,140 @@ def tile_picked_tokmax_none_po_kernel(
         xb_s = pick(xs[:], two_t, sb([P, S], U8, "xb_s"))
         xa_s = pick(xs[:], offs_t, sb([P, S], U8, "xa_s"))
 
-        def staged(name, offset):
-            return placed.tile([P, HALF * PACK], BF16, name=name, offset=offset, align_bytes=64)
-
-        wb_g = [placed.tile([P, HALF * PACK], BF16, name="wb_g0", offset=2 * S, align_bytes=64), staged("wb_g1", 4096 + 2048)]
+        wb_g = [at(1, [P, HALF * PACK], BF16, "wb_g0"), at(11, [P, HALF * PACK], BF16, "wb_g1")]
         wb_c = sb([P, H], U32, "wb_c")
         wb_s = sb([P, H], U8, "wb_s")
-        wa_s = [sb([P, HALF], U8, "wa_s%d" % h) for h in range(2)]
-        cast(nc.scalar.copy, wb_raw[0][:], wb_g[0][:])
-        cast(nc.scalar.copy, wb_raw[1][:], wb_g[1][:])
-
-        def rows(t):
-            return slice(t * P, (t + 1) * P)
-
-        def project(acc, x_w, x_s, t, w_c, w_s):
-            nc.tensor.matmul_mx(
-                out=acc, lhsT=x_w[:, rows(t)].bitcast(FP8X4), lhsT_scale=x_s[:, rows(t)],
-                rhs=w_c.bitcast(FP8X4), rhs_scale=w_s, start=True, stop=True,
-            )
-
-        b_acc = [[bank(4 * (1 - h) + t, [P, HALF], "b_acc%d_%d" % (h, t)) for t in range(PACK)] for h in range(2)]
-        quantize(wb_c[:, 0:HALF], wb_s[:, 0:HALF], wb_g[0][:])
-        xb_w = pick(xw[:].bitcast(U32), two_t, placed.tile([P, S], U32, name="xb_w", offset=0, align_bytes=64))
-        xa_w = pick(xw[:].bitcast(U32), offs_t, placed.tile([P, S], U32, name="xa_w", offset=4 * S, align_bytes=64))
-        quantize(wb_c[:, HALF:H], wb_s[:, HALF:H], wb_g[1][:])
         for h in range(2):
-            cols = slice(h * HALF, (h + 1) * HALF)
+            cast(nc.scalar.copy, wb_raw[h][:], wb_g[h][:])
+        quantize(wb_c[:, half(0)], wb_s[:, half(0)], wb_g[0][:])
+        xb_w = pick(xw[:].bitcast(U32), two_t, at(0, [P, S], U32, "xb_w"))
+        xa_w = pick(xw[:].bitcast(U32), offs_t, at(2, [P, S], U32, "xa_w"))
+        quantize(wb_c[:, half(1)], wb_s[:, half(1)], wb_g[1][:])
+
+        b_acc = [[bank(PACK * (1 - h) + t, [P, HALF], "b_acc%d_%d" % (h, t)) for t in range(PACK)] for h in range(2)]
+        for h in range(2):
             for t in range(PACK):
-                project(b_acc[h][t][:], xb_w, xb_s, t, wb_c[:, cols], wb_s[:, cols])
+                project(b_acc[h][t][:], xb_w, xb_s, t, wb_c[:, half(h)], wb_s[:, half(h)])
 
-        b_at = [10240 + 512, 10240 + 2560, 10240 + 4608, 4096 + 256]
-        b_sb = [placed.tile([P, H], F32, name="b_sb%d" % t, offset=b_at[t], align_bytes=64) for t in range(PACK)]
+        b_sb = [at(4 + 2 * t, [P, H], F32, "b_sb%d" % t) for t in range(PACK)]
 
-        def copy_b(h, t):
-            copy = nc.vector.tensor_copy if t == 3 or (h, t) == (1, 1) else nc.scalar.copy
-            copy(out=b_sb[t][:, h * HALF : (h + 1) * HALF], in_=b_acc[h][t][:])
+        def copy_b(copy, h, t):
+            copy(out=b_sb[t][:, half(h)], in_=b_acc[h][t][:])
 
         def cast_wa(h):
-            wa_g = staged("wa_g%d" % h, 4096 + 2304)
+            wa_g = at(12, [P, HALF * PACK], BF16, "wa_g%d" % h)
             nc.gpsimd.tensor_scalar(
                 out=wa_g[:].rearrange("p (c j) -> p c j", j=PACK), in0=wa_raw[h][:].rearrange("p j c -> p c j"),
                 scalar1=1.0, scalar2=0.0, op0=ALU.mult, op1=ALU.add,
             )
             return wa_g
 
-        def project_a(h, wa_g, tag):
-            wa_c = keep.tile([P, HALF], U32, name="wa_c%d" % h, tag=tag, align_bytes=64)
-            quantize(wa_c[:], wa_s[h][:], wa_g[:])
-            accs = [bank(4 + 2 * h + u, [P, 2, HALF], "a_acc%d_%d" % (h, u)) for u in range(2)]
-            for t in range(PACK):
-                project(accs[t // 2][:, t % 2, :], xa_w, xa_s, t, wa_c[:], wa_s[h][:])
+        def project_a(h, wa_g, wa_c):
+            wa_s = sb([P, HALF], U8, "wa_s%d" % h)
+            quantize(wa_c[:], wa_s[:], wa_g[:])
+            accs = [bank(PACK + 2 * h + u, [P, 2, HALF], "a_acc%d_%d" % (h, u)) for u in range(2)]
+            for u, pair in enumerate(PAIRS):
+                for v, t in enumerate(pair):
+                    project(accs[u][:, v, :], xa_w, xa_s, t, wa_c[:], wa_s[:])
             return accs
 
-        def pair_slot(h, u):
-            return keep.tile([P, 2, HALF], F32, name="bq%d_%d" % (h, u), tag="bq%d_%d" % (h, u), align_bytes=64)
-
-        bq = [[pair_slot(0, u) for u in range(2)]]
-
         def picked_b(h, t):
-            return bq[h][t // 2][:, t % 2, :], b_sb[t][:].indirect(fl_t[:, h * HALF // 16 : (h + 1) * HALF // 16])
+            return b_sb[t][:].indirect(fl_t[:, h * HALF // 16 : (h + 1) * HALF // 16])
 
-        def gather_on_scalar(h, t):
-            out, picked = picked_b(h, t)
-            nc.scalar.activation(out=out, in_=picked, func=ACT.Copy)
+        def gather_on_scalar(bq, h, t):
+            nc.scalar.activation(out=bq[t % 2][:, t // 2, :], in_=picked_b(h, t), func=ACT.Copy)
 
-        def gather_on_vector(h, t):
-            nc.vector.tensor_copy(*picked_b(h, t))
-
-        def larger(h, accs, picked):
-            m = keep.tile([P, PACK, HALF], F32, name="m%d" % h, tag="m", align_bytes=64)
+        def larger(h, accs, bq):
+            m = slot("m", [P, PACK, HALF], F32, "m%d" % h)
             for u in range(2):
-                nc.vector.tensor_tensor(out=m[:, 2 * u : 2 * u + 2, :], in0=accs[u][:], in1=picked[u][:], op=ALU.max)
+                nc.vector.tensor_tensor(out=m[:, u:PACK:2, :], in0=accs[u][:], in1=bq[u][:], op=ALU.max)
             return m
 
-        def weigh(name, m_ap):
-            width = m_ap.shape[2]
-            z = keep.tile([P, width * PACK], BF16, name=name, tag=name, align_bytes=64)
+        def weigh(c, m):
+            z = slot("z%d" % c, [P, CHUNK * PACK], BF16, "z%d" % c)
             nc.vector.tensor_tensor(
-                out=woven(z[:]), in0=walk(m_ap),
-                in1=g[:].unsqueeze(1).unsqueeze(3).to_broadcast([P, width // LINE, PACK, LINE]), op=ALU.mult,
+                out=woven(z[:]), in0=walk(m[:, :, chunk(c % 2)]),
+                in1=g[:].unsqueeze(1).unsqueeze(3).to_broadcast([P, CHUNK // LINE, PACK, LINE]), op=ALU.mult,
             )
             return z
 
-        def quantize_z(name, z, tag):
-            z_c = keep.tile([P, CHUNK], U32, name=name + "_c", tag=tag, align_bytes=64)
-            z_s = sb([P, CHUNK], U8, name + "_s")
-            quantize(z_c[:], z_s[:], z)
+        def quantize_z(c, z, z_c):
+            z_s = sb([P, CHUNK], U8, "z_s%d" % c)
+            quantize(z_c[:], z_s[:], z[:])
             return z_c, z_s
 
         out_v = out_0.rearrange("(p t) j -> p t j", t=PACK)
         words_v = out_1[0].rearrange("p n r -> p (n r)").bitcast(I32)
+        y_g = sb([P, H * PACK], BF16, "y_g")
         y_s = sb([P, H], U8, "y_s")
 
-        def mix(first, width, banks, z_c, z_s, copies):
-            y = sb([P, PACK, width], F32, "y%d" % first)
-            per = PACK // len(banks)
-            for u, which in enumerate(banks):
-                acc = bank(which, [P, per, width], "y_acc%d" % which)
+        def mix(c, z_q, emptied):
+            z_c, z_s = z_q
+            y = sb([P, PACK, CHUNK], F32, "y%d" % c)
+            per = PACK // len(emptied)
+            for u, (which, copy) in enumerate(emptied):
+                acc = bank(which, [P, per, CHUNK], "y_acc%d" % which)
                 for v in range(per):
                     t = u * per + v
                     nc.tensor.matmul_mx(
                         out=acc[:, v, :], lhsT=w1w_d[:, 2 * P * t : 2 * P * (t + 1)].bitcast(FP4X4), lhsT_scale=w1s_d[:, rows(t)],
-                        rhs=z_c.bitcast(FP8X4), rhs_scale=z_s, start=True, stop=True,
+                        rhs=z_c[:].bitcast(FP8X4), rhs_scale=z_s[:], start=True, stop=True,
                     )
-                copies[u](out=y[:, u * per : (u + 1) * per, :], in_=acc[:])
-            nc.sync.dma_start(out=out_v[:, :, first : first + width], in_=y[:])
+                copy(out=y[:, u * per : (u + 1) * per, :], in_=acc[:])
+            nc.sync.dma_start(out=out_v[:, :, chunk(c)], in_=y[:])
             return y
 
-        yg = sb([P, H * PACK], BF16, "yg")
+        def round_y(copy, c, y):
+            cast(copy, y[:], y_g[:, chunk(c, PACK)])
 
-        def round_y(first, y, copy):
-            cast(copy, y[:], yg[:, first * PACK : (first + y.shape[2]) * PACK])
-
-        def quantize_y(y_c, first, last):
-            cols = slice(first * CHUNK, last * CHUNK)
-            quantize(y_c[:, cols], y_s[:, cols], yg[:, first * CHUNK * PACK : last * CHUNK * PACK])
+        on_scalar, on_vector = nc.scalar.copy, nc.vector.tensor_copy
 
         wa_g0 = cast_wa(0)
         for t in range(PACK):
-            copy_b(0, t)
-        for t in range(3):
-            copy_b(1, t)
-        a0 = project_a(0, wa_g0, "wa_c0")
-        wa_g1 = cast_wa(1)
-        copy_b(1, 3)
-        gather_on_vector(0, 1)
-        for t in (0, 2, 3):
-            gather_on_scalar(0, t)
-        m0 = larger(0, a0, bq[0])
-        a1 = project_a(1, wa_g1, "bq0_0")
-        bq.append([pair_slot(1, u) for u in range(2)])
+            copy_b(on_vector if t == PACK - 1 else on_scalar, 0, t)
         for t in range(PACK):
-            gather_on_scalar(1, t)
-        z01 = weigh("z01", m0[:])
-        w1s_d = keep.tile([P, N], U8, name="w1s_d", tag="bq0_1", align_bytes=64)
+            copy_b(on_vector if t % 2 else on_scalar, 1, t)
+        a0 = project_a(0, wa_g0, sb([P, HALF], U32, "wa_c0"))
+        wa_g1 = cast_wa(1)
+
+        bq0 = [slot("bq00", [P, 2, HALF], F32, "bq00"), at(14, [P, 2, HALF], F32, "bq01")]
+        nc.vector.tensor_copy(bq0[1][:, 0, :], picked_b(0, 1))
+        for t in (0, 2, 3):
+            gather_on_scalar(bq0, 0, t)
+        m0 = larger(0, a0, bq0)
+
+        a1 = project_a(1, wa_g1, slot("bq00", [P, HALF], U32, "wa_c1"))
+        bq1 = [at(16 + 2 * u, [P, 2, HALF], F32, "bq1%d" % u) for u in range(2)]
+        for pair in PAIRS:
+            for t in pair:
+                gather_on_scalar(bq1, 1, t)
+        w1s_d = at(14, [P, N], U8, "w1s_d")
         nc.vector.tensor_copy(
             out=w1s_d[:].rearrange("p (t m) -> p t m", t=PACK), in_=w1s[:].rearrange("p (m t) -> p t m", t=PACK)
         )
-        zq0 = quantize_z("zq0", z01[:, 0 : CHUNK * PACK], "zq0")
-        y0 = mix(0, CHUNK, (0,), zq0[0][:], zq0[1][:], [nc.scalar.copy])
-        round_y(0, y0, nc.scalar.copy)
-        m1 = larger(1, a1, bq[1])
-        zq1 = quantize_z("zq1", z01[:, CHUNK * PACK : HALF * PACK], "bq1_0")
-        y1 = mix(CHUNK, CHUNK, (1,), zq1[0][:], zq1[1][:], [nc.scalar.copy])
-        z2 = weigh("z2", m1[:, :, 0:CHUNK])
-        z3 = weigh("z3", m1[:, :, CHUNK:HALF])
-        zq2 = quantize_z("zq2", z2[:], "zq2")
-        zq3 = quantize_z("zq3", z3[:], "zq3")
-        both = [nc.scalar.copy, nc.vector.tensor_copy]
-        y2 = mix(HALF, CHUNK, (2, 3), zq2[0][:], zq2[1][:], both)
-        y3 = mix(HALF + CHUNK, CHUNK, (4, 5), zq3[0][:], zq3[1][:], [nc.scalar.copy] * 2)
-        y_c = keep.tile([P, H], I32, name="y_c", tag="z3", align_bytes=64)
-        round_y(CHUNK, y1, nc.vector.tensor_copy)
-        quantize_y(y_c, 0, 2)
-        nc.sync.dma_start(out=words_v[:, 0:HALF], in_=y_c[:, 0:HALF])
-        round_y(HALF, y2, nc.vector.tensor_copy)
-        round_y(HALF + CHUNK, y3, nc.vector.tensor_copy)
-        quantize_y(y_c, 2, 3)
-        quantize_y(y_c, 3, 4)
-        nc.sync.dma_start(out=words_v[:, HALF:H], in_=y_c[:, HALF:H])
+        z0 = weigh(0, m0)
+        z1 = weigh(1, m0)
+        y0 = mix(0, quantize_z(0, z0, sb([P, CHUNK], U32, "z_c0")), [(0, on_scalar)])
+        round_y(on_scalar, 0, y0)
+
+        m1 = larger(1, a1, bq1)
+        y1 = mix(1, quantize_z(1, z1, at(16, [P, CHUNK], U32, "z_c1")), [(1, on_scalar)])
+        z2 = weigh(2, m1)
+        z3 = weigh(3, m1)
+        z_q2 = quantize_z(2, z2, sb([P, CHUNK], U32, "z_c2"))
+        z_q3 = quantize_z(3, z3, sb([P, CHUNK], U32, "z_c3"))
+        y2 = mix(2, z_q2, [(2, on_scalar), (3, on_vector)])
+        y3 = mix(3, z_q3, [(4, on_scalar), (5, on_scalar)])
+
+        y_c = slot("z3", [P, H], I32, "y_c")
+        round_y(on_vector, 1, y1)
+        quantize(y_c[:, half(0)], y_s[:, half(0)], y_g[:, 0 : HALF * PACK])
+        nc.sync.dma_start(out=words_v[:, half(0)], in_=y_c[:, half(0)])
+        round_y(on_vector, 2, y2)
+        round_y(on_vector, 3, y3)
+        for c in (2, 3):
+            quantize(y_c[:, chunk(c)], y_s[:, chunk(c)], y_g[:, chunk(c, PACK)])
+        nc.sync.dma_start(out=words_v[:, half(1)], in_=y_c[:, half(1)])
         for q in range(4):
             eng = nc.scalar if q % 2 else nc.sync
             eng.dma_start(out=out_2[0, 4 * q : 4 * q + 4, :].bitcast(I32), in_=y_s[32 * q : 32 * q + 4, :].bitcast(I32))

@@ -237,6 +237,8 @@ def tile_picked_tokmax_none_po_kernel(
         round_y(on_scalar, 0, y0)
 
         m1 = larger(1, a1, bq1)
+        warm = bank(6, [P, H], "warm")
+        project(warm[:], wb_c, wb_s, 0, wb_c[:], wb_s[:])
         y1 = mix(1, quantize_z(1, z1, at(16, [P, CHUNK], U32, "z_c1")), [(1, on_scalar)])
         z2 = weigh(2, m1)
         z3 = weigh(3, m1)

@@ -148,26 +148,19 @@ def tile_picked_tokmax_none_po_kernel(
             )
             return wa_g
 
-        def project_a(h, wa_g, wa_c):
+        def quantize_wa(h, wa_g, wa_c):
             wa_s = sb([P, HALF], U8, "wa_s%d" % h)
             quantize(wa_c[:], wa_s[:], wa_g[:])
-            accs = [bank(PACK + 2 * h + u, [P, 2, HALF], "a_acc%d_%d" % (h, u)) for u in range(2)]
-            for u, pair in enumerate(PAIRS):
-                for v, t in enumerate(pair):
-                    project(accs[u][:, v, :], xa_w, xa_s, t, wa_c[:], wa_s[:])
-            return accs
+            return wa_c, wa_s
 
         def picked_b(h, t):
             return b_sb[t][:].indirect(fl_t[:, h * HALF // 16 : (h + 1) * HALF // 16])
 
-        def gather_on_scalar(bq, h, t):
-            nc.scalar.activation(out=bq[t % 2][:, t // 2, :], in_=picked_b(h, t), func=ACT.Copy)
+        def gather_on_scalar(out, h, t):
+            nc.scalar.activation(out=out, in_=picked_b(h, t), func=ACT.Copy)
 
-        def larger(h, accs, bq):
-            m = slot("m", [P, PACK, HALF], F32, "m%d" % h)
-            for u in range(2):
-                nc.vector.tensor_tensor(out=m[:, u:PACK:2, :], in0=accs[u][:], in1=bq[u][:], op=ALU.max)
-            return m
+        def larger(out, acc, bq_ap):
+            nc.vector.tensor_tensor(out=out, in0=acc[:], in1=bq_ap, op=ALU.max)
 
         def weigh(c, m):
             z = slot("z%d" % c, [P, CHUNK * PACK], BF16, "z%d" % c)
@@ -213,20 +206,29 @@ def tile_picked_tokmax_none_po_kernel(
             copy_b(on_vector if t == PACK - 1 else on_scalar, 0, t)
         for t in range(PACK):
             copy_b(on_vector if t % 2 else on_scalar, 1, t)
-        a0 = project_a(0, wa_g0, sb([P, HALF], U32, "wa_c0"))
+        wa_c, wa_s = quantize_wa(0, wa_g0, sb([P, HALF], U32, "wa_c0"))
+        a0 = [bank(PACK + u, [P, 2, HALF], "a_pair%d" % u) for u in range(2)]
+        for u, pair in enumerate(PAIRS):
+            for v, t in enumerate(pair):
+                project(a0[u][:, v, :], xa_w, xa_s, t, wa_c[:], wa_s[:])
         wa_g1 = cast_wa(1)
 
         bq0 = [slot("bq00", [P, 2, HALF], F32, "bq00"), at(14, [P, 2, HALF], F32, "bq01")]
         nc.vector.tensor_copy(bq0[1][:, 0, :], picked_b(0, 1))
         for t in (0, 2, 3):
-            gather_on_scalar(bq0, 0, t)
-        m0 = larger(0, a0, bq0)
+            gather_on_scalar(bq0[t % 2][:, t // 2, :], 0, t)
+        m0 = slot("m", [P, PACK, HALF], F32, "m0")
+        for u in range(2):
+            larger(m0[:, u:PACK:2, :], a0[u], bq0[u][:])
 
-        a1 = project_a(1, wa_g1, slot("bq00", [P, HALF], U32, "wa_c1"))
-        bq1 = [at(16 + 2 * u, [P, 2, HALF], F32, "bq1%d" % u) for u in range(2)]
-        for pair in PAIRS:
-            for t in pair:
-                gather_on_scalar(bq1, 1, t)
+        wa_c, wa_s = quantize_wa(1, wa_g1, slot("bq00", [P, HALF], U32, "wa_c1"))
+        a1 = [bank(PACK + 2 + u, [P, PACK, CHUNK], "a_chunk%d" % u) for u in range(2)]
+        for u in range(2):
+            for t in range(PACK):
+                project(a1[u][:, t, :], xa_w, xa_s, t, wa_c[:, chunk(u)], wa_s[:, chunk(u)])
+        bq1 = at(16, [P, PACK, HALF], F32, "bq1")
+        for t in range(PACK):
+            gather_on_scalar(bq1[:, t, :], 1, t)
         w1s_d = at(14, [P, N], U8, "w1s_d")
         nc.vector.tensor_copy(
             out=w1s_d[:].rearrange("p (t m) -> p t m", t=PACK), in_=w1s[:].rearrange("p (m t) -> p t m", t=PACK)
@@ -234,12 +236,15 @@ def tile_picked_tokmax_none_po_kernel(
         z0 = weigh(0, m0)
         z1 = weigh(1, m0)
         y0 = mix(0, quantize_z(0, z0, sb([P, CHUNK], U32, "z_c0")), [(0, on_scalar)])
+        y1 = mix(1, quantize_z(1, z1, sb([P, CHUNK], U32, "z_c1")), [(1, on_scalar)])
         round_y(on_scalar, 0, y0)
+        round_y(on_scalar, 1, y1)
 
-        m1 = larger(1, a1, bq1)
-        warm = bank(6, [P, H], "warm")
+        m1 = slot("m", [P, PACK, HALF], F32, "m1")
+        for u in range(2):
+            larger(m1[:, :, chunk(u)], a1[u], bq1[:, :, chunk(u)])
+        warm = bank(7, [P, H], "warm")
         project(warm[:], wb_c, wb_s, 0, wb_c[:], wb_s[:])
-        y1 = mix(1, quantize_z(1, z1, at(16, [P, CHUNK], U32, "z_c1")), [(1, on_scalar)])
         z2 = weigh(2, m1)
         z3 = weigh(3, m1)
         z_q2 = quantize_z(2, z2, sb([P, CHUNK], U32, "z_c2"))
@@ -248,7 +253,6 @@ def tile_picked_tokmax_none_po_kernel(
         y3 = mix(3, z_q3, [(4, on_scalar), (5, on_scalar)])
 
         y_c = slot("z3", [P, H], I32, "y_c")
-        round_y(on_vector, 1, y1)
         quantize(y_c[:, half(0)], y_s[:, half(0)], y_g[:, 0 : HALF * PACK])
         nc.sync.dma_start(out=words_v[:, half(0)], in_=y_c[:, half(0)])
         round_y(on_vector, 2, y2)

@@ -180,9 +180,8 @@ def tile_picked_tokmax_none_po_kernel(
         y_g = sb([P, H * PACK], BF16, "y_g")
         y_s = sb([P, H], U8, "y_s")
 
-        def mix(c, z_q, emptied):
+        def mix(c, z_q, emptied, y):
             z_c, z_s = z_q
-            y = sb([P, PACK, CHUNK], F32, "y%d" % c)
             per = PACK // len(emptied)
             for u, (which, copy) in enumerate(emptied):
                 acc = bank(which, [P, per, CHUNK], "y_acc%d" % which)
@@ -193,11 +192,9 @@ def tile_picked_tokmax_none_po_kernel(
                         rhs=z_c[:].bitcast(FP8X4), rhs_scale=z_s[:], start=True, stop=True,
                     )
                 copy(out=y[:, u * per : (u + 1) * per, :], in_=acc[:])
-            nc.sync.dma_start(out=out_v[:, :, chunk(c)], in_=y[:])
-            return y
 
         def round_y(copy, c, y):
-            cast(copy, y[:], y_g[:, chunk(c, PACK)])
+            cast(copy, y, y_g[:, chunk(c, PACK)])
 
         on_scalar, on_vector = nc.scalar.copy, nc.vector.tensor_copy
 
@@ -235,10 +232,12 @@ def tile_picked_tokmax_none_po_kernel(
         )
         z0 = weigh(0, m0)
         z1 = weigh(1, m0)
-        y0 = mix(0, quantize_z(0, z0, sb([P, CHUNK], U32, "z_c0")), [(0, on_scalar)])
-        y1 = mix(1, quantize_z(1, z1, sb([P, CHUNK], U32, "z_c1")), [(1, on_scalar)])
-        round_y(on_scalar, 0, y0)
-        round_y(on_scalar, 1, y1)
+        y01 = sb([P, PACK, HALF], F32, "y01")
+        for c, z in enumerate((z0, z1)):
+            mix(c, quantize_z(c, z, sb([P, CHUNK], U32, "z_c%d" % c)), [(c, on_scalar)], y01[:, :, chunk(c)])
+        nc.sync.dma_start(out=out_v[:, :, half(0)], in_=y01[:])
+        for c in range(2):
+            round_y(on_scalar, c, y01[:, :, chunk(c)])
 
         m1 = slot("m", [P, PACK, HALF], F32, "m1")
         for u in range(2):
@@ -249,17 +248,21 @@ def tile_picked_tokmax_none_po_kernel(
         z3 = weigh(3, m1)
         z_q2 = quantize_z(2, z2, sb([P, CHUNK], U32, "z_c2"))
         z_q3 = quantize_z(3, z3, sb([P, CHUNK], U32, "z_c3"))
-        y2 = mix(2, z_q2, [(2, on_scalar), (3, on_vector)])
-        y3 = mix(3, z_q3, [(4, on_scalar), (5, on_scalar)])
+        y2 = sb([P, PACK, CHUNK], F32, "y2")
+        y3 = sb([P, PACK, CHUNK], F32, "y3")
+        mix(2, z_q2, [(2, on_scalar), (3, on_vector)], y2[:])
+        for u in range(2):
+            nc.sync.dma_start(out=out_v[:, 2 * u : 2 * u + 2, chunk(2)], in_=y2[:, 2 * u : 2 * u + 2, :])
+        mix(3, z_q3, [(4, on_scalar), (5, on_scalar)], y3[:])
+        nc.sync.dma_start(out=out_v[:, :, chunk(3)], in_=y3[:])
 
         y_c = slot("z3", [P, H], I32, "y_c")
         quantize(y_c[:, half(0)], y_s[:, half(0)], y_g[:, 0 : HALF * PACK])
-        nc.sync.dma_start(out=words_v[:, half(0)], in_=y_c[:, half(0)])
-        round_y(on_vector, 2, y2)
-        round_y(on_vector, 3, y3)
+        round_y(on_vector, 2, y2[:])
+        round_y(on_vector, 3, y3[:])
         for c in (2, 3):
             quantize(y_c[:, chunk(c)], y_s[:, chunk(c)], y_g[:, chunk(c, PACK)])
-        nc.sync.dma_start(out=words_v[:, half(1)], in_=y_c[:, half(1)])
+        nc.sync.dma_start(out=words_v, in_=y_c[:])
         for q in range(4):
             eng = nc.scalar if q % 2 else nc.sync
             eng.dma_start(out=out_2[0, 4 * q : 4 * q + 4, :].bitcast(I32), in_=y_s[32 * q : 32 * q + 4, :].bitcast(I32))

@@ -242,8 +242,6 @@ def tile_picked_tokmax_none_po_kernel(
         m1 = slot("m", [P, PACK, HALF], F32, "m1")
         for u in range(2):
             larger(m1[:, :, chunk(u)], a1[u], bq1[:, :, chunk(u)])
-        warm = bank(7, [P, H], "warm")
-        project(warm[:], wb_c, wb_s, 0, wb_c[:], wb_s[:])
         z2 = weigh(2, m1)
         z3 = weigh(3, m1)
         z_q2 = quantize_z(2, z2, sb([P, CHUNK], U32, "z_c2"))

@@ -22,6 +22,7 @@ HALF = H // 2
 CHUNK = 128
 LINE = 4
 KIB = 1024
+WB_ON_SCALAR = (160, 208)
 PAIRS = ((0, 2), (1, 3))
 
 
@@ -55,7 +56,7 @@ def tile_picked_tokmax_none_po_kernel(
         w1s = sb([P, N], U8, "w1s")
         g = sb([P, PACK], F32, "g")
 
-        wb_raw = [sb([P, PACK, HALF], F32, "wb_raw0"), at(5, [P, PACK, HALF], F32, "wb_raw1")]
+        wb_raw = [at(4 * h, [P, PACK, HALF], F32, "wb_raw%d" % h) for h in range(2)]
         wa_raw = [at(15, [P, PACK, HALF], F32, "wa_raw0"), sb([P, PACK, HALF], F32, "wa_raw1")]
 
         nc.vector.memset(xs[:].bitcast(I32), 0)
@@ -68,12 +69,12 @@ def tile_picked_tokmax_none_po_kernel(
             for q in range(4):
                 queues[q].dma_start(out=dst[32 * q : 32 * q + 4, :].bitcast(I32), in_=src[0, 4 * q : 4 * q + 4, :].bitcast(I32))
 
-        nc.sync.dma_start(out=w1w[:].bitcast(I32), in_=w1_words[0].bitcast(I32))
+        nc.scalar.dma_start(out=w1w[:].bitcast(I32), in_=w1_words[0].bitcast(I32))
         nc.sync.dma_start(two_t[:], two)
-        nc.sync.dma_start(offs_t[:], offs)
-        load_scale_rows(xs, x_scales, (nc.sync, nc.sync, nc.scalar, nc.scalar))
-        nc.sync.dma_start(out=wb_raw[0][:], in_=wb_v[:, :, 0:HALF])
         nc.sync.dma_start(out=xw[:], in_=x_words[0].rearrange("p n t -> p (n t)").bitcast(I32))
+        nc.sync.dma_start(offs_t[:], offs)
+        load_scale_rows(xs, x_scales, (nc.sync,) * 4)
+        nc.sync.dma_start(out=wb_raw[0][:], in_=wb_v[:, :, 0:HALF])
         nc.sync.dma_start(out=wb_raw[1][:], in_=wb_v[:, :, HALF:H])
         nc.sync.dma_start(out=wa_raw[0][:], in_=wa_v[:, :, 0:HALF])
         nc.sync.dma_start(fl_t[:], fl)
@@ -117,25 +118,30 @@ def tile_picked_tokmax_none_po_kernel(
             out=w1w_d[:].rearrange("p (t m b) -> p t m b", t=PACK, b=2),
             in_=w1w[:].rearrange("p (m t b) -> p t m b", t=PACK, b=2),
         )
+        xb_w = pick(xw[:].bitcast(U32), two_t, sb([P, S], U32, "xb_w"))
         xb_s = pick(xs[:], two_t, sb([P, S], U8, "xb_s"))
-        xa_s = pick(xs[:], offs_t, sb([P, S], U8, "xa_s"))
 
-        wb_g = [at(1, [P, HALF * PACK], BF16, "wb_g0"), at(11, [P, HALF * PACK], BF16, "wb_g1")]
+        wb_g = [sb([P, HALF * PACK], BF16, "wb_g0"), at(11, [P, HALF * PACK], BF16, "wb_g1")]
         wb_c = sb([P, H], U32, "wb_c")
         wb_s = sb([P, H], U8, "wb_s")
-        for h in range(2):
-            cast(nc.scalar.copy, wb_raw[h][:], wb_g[h][:])
-        quantize(wb_c[:, half(0)], wb_s[:, half(0)], wb_g[0][:])
-        xb_w = pick(xw[:].bitcast(U32), two_t, at(0, [P, S], U32, "xb_w"))
-        xa_w = pick(xw[:].bitcast(U32), offs_t, at(2, [P, S], U32, "xa_w"))
-        quantize(wb_c[:, half(1)], wb_s[:, half(1)], wb_g[1][:])
+
+        def quantize_wb(h):
+            n = WB_ON_SCALAR[h]
+            cast(nc.scalar.copy, wb_raw[h][:, :, 0:n], wb_g[h][:, 0 : n * PACK])
+            cast(nc.vector.tensor_copy, wb_raw[h][:, :, n:HALF], wb_g[h][:, n * PACK : HALF * PACK])
+            quantize(wb_c[:, half(h)], wb_s[:, half(h)], wb_g[h][:])
+
+        quantize_wb(0)
+        xa_s = pick(xs[:], offs_t, at(0, [P, S], U8, "xa_s"))
+        quantize_wb(1)
+        xa_w = pick(xw[:].bitcast(U32), offs_t, at(4, [P, S], U32, "xa_w"))
 
         b_acc = [[bank(PACK * (1 - h) + t, [P, HALF], "b_acc%d_%d" % (h, t)) for t in range(PACK)] for h in range(2)]
         for h in range(2):
             for t in range(PACK):
                 project(b_acc[h][t][:], xb_w, xb_s, t, wb_c[:, half(h)], wb_s[:, half(h)])
 
-        b_sb = [at(4 + 2 * t, [P, H], F32, "b_sb%d" % t) for t in range(PACK)]
+        b_sb = [sb([P, H], F32, "b_sb%d" % t) for t in range(PACK)]
 
         def copy_b(copy, h, t):
             copy(out=b_sb[t][:, half(h)], in_=b_acc[h][t][:])
@@ -200,7 +206,7 @@ def tile_picked_tokmax_none_po_kernel(
 
         wa_g0 = cast_wa(0)
         for t in range(PACK):
-            copy_b(on_vector if t == PACK - 1 else on_scalar, 0, t)
+            copy_b(on_scalar, 0, t)
         for t in range(PACK):
             copy_b(on_vector if t % 2 else on_scalar, 1, t)
         wa_c, wa_s = quantize_wa(0, wa_g0, sb([P, HALF], U32, "wa_c0"))

@@ -22,7 +22,7 @@ HALF = H // 2
 CHUNK = 128
 LINE = 4
 KIB = 1024
-WB_ON_SCALAR = (160, 208)
+WB_ON_SCALAR = (256, 112)
 PAIRS = ((0, 2), (1, 3))
 
 
@@ -57,7 +57,7 @@ def tile_picked_tokmax_none_po_kernel(
         g = sb([P, PACK], F32, "g")
 
         wb_raw = [at(4 * h, [P, PACK, HALF], F32, "wb_raw%d" % h) for h in range(2)]
-        wa_raw = [at(15, [P, PACK, HALF], F32, "wa_raw0"), sb([P, PACK, HALF], F32, "wa_raw1")]
+        wa_raw = [at(21, [P, PACK, HALF], F32, "wa_raw0"), sb([P, PACK, HALF], F32, "wa_raw1")]
 
         nc.vector.memset(xs[:].bitcast(I32), 0)
         nc.vector.memset(w1s[:].bitcast(I32), 0)
@@ -69,12 +69,12 @@ def tile_picked_tokmax_none_po_kernel(
             for q in range(4):
                 queues[q].dma_start(out=dst[32 * q : 32 * q + 4, :].bitcast(I32), in_=src[0, 4 * q : 4 * q + 4, :].bitcast(I32))
 
-        nc.scalar.dma_start(out=w1w[:].bitcast(I32), in_=w1_words[0].bitcast(I32))
+        nc.sync.dma_start(out=w1w[:].bitcast(I32), in_=w1_words[0].bitcast(I32))
         nc.sync.dma_start(two_t[:], two)
-        nc.sync.dma_start(out=xw[:], in_=x_words[0].rearrange("p n t -> p (n t)").bitcast(I32))
         nc.sync.dma_start(offs_t[:], offs)
-        load_scale_rows(xs, x_scales, (nc.sync,) * 4)
+        load_scale_rows(xs, x_scales, (nc.sync, nc.sync, nc.scalar, nc.scalar))
         nc.sync.dma_start(out=wb_raw[0][:], in_=wb_v[:, :, 0:HALF])
+        nc.sync.dma_start(out=xw[:], in_=x_words[0].rearrange("p n t -> p (n t)").bitcast(I32))
         nc.sync.dma_start(out=wb_raw[1][:], in_=wb_v[:, :, HALF:H])
         nc.sync.dma_start(out=wa_raw[0][:], in_=wa_v[:, :, 0:HALF])
         nc.sync.dma_start(fl_t[:], fl)
@@ -118,21 +118,22 @@ def tile_picked_tokmax_none_po_kernel(
             out=w1w_d[:].rearrange("p (t m b) -> p t m b", t=PACK, b=2),
             in_=w1w[:].rearrange("p (m t b) -> p t m b", t=PACK, b=2),
         )
-        xb_w = pick(xw[:].bitcast(U32), two_t, sb([P, S], U32, "xb_w"))
         xb_s = pick(xs[:], two_t, sb([P, S], U8, "xb_s"))
+        xa_s = pick(xs[:], offs_t, sb([P, S], U8, "xa_s"))
 
         wb_g = [sb([P, HALF * PACK], BF16, "wb_g0"), at(11, [P, HALF * PACK], BF16, "wb_g1")]
-        wb_c = sb([P, H], U32, "wb_c")
+        wb_c = at(19, [P, H], U32, "wb_c")
         wb_s = sb([P, H], U8, "wb_s")
 
         def quantize_wb(h):
             n = WB_ON_SCALAR[h]
             cast(nc.scalar.copy, wb_raw[h][:, :, 0:n], wb_g[h][:, 0 : n * PACK])
-            cast(nc.vector.tensor_copy, wb_raw[h][:, :, n:HALF], wb_g[h][:, n * PACK : HALF * PACK])
+            if n < HALF:
+                cast(nc.vector.tensor_copy, wb_raw[h][:, :, n:HALF], wb_g[h][:, n * PACK : HALF * PACK])
             quantize(wb_c[:, half(h)], wb_s[:, half(h)], wb_g[h][:])
 
         quantize_wb(0)
-        xa_s = pick(xs[:], offs_t, at(0, [P, S], U8, "xa_s"))
+        xb_w = pick(xw[:].bitcast(U32), two_t, at(0, [P, S], U32, "xb_w"))
         quantize_wb(1)
         xa_w = pick(xw[:].bitcast(U32), offs_t, at(4, [P, S], U32, "xa_w"))
 
@@ -147,7 +148,7 @@ def tile_picked_tokmax_none_po_kernel(
             copy(out=b_sb[t][:, half(h)], in_=b_acc[h][t][:])
 
         def cast_wa(h):
-            wa_g = at(12, [P, HALF * PACK], BF16, "wa_g%d" % h)
+            wa_g = at(12 - h, [P, HALF * PACK], BF16, "wa_g%d" % h)
             nc.gpsimd.tensor_scalar(
                 out=wa_g[:].rearrange("p (c j) -> p c j", j=PACK), in0=wa_raw[h][:].rearrange("p j c -> p c j"),
                 scalar1=1.0, scalar2=0.0, op0=ALU.mult, op1=ALU.add,
@@ -209,14 +210,14 @@ def tile_picked_tokmax_none_po_kernel(
             copy_b(on_scalar, 0, t)
         for t in range(PACK):
             copy_b(on_vector if t % 2 else on_scalar, 1, t)
-        wa_c, wa_s = quantize_wa(0, wa_g0, sb([P, HALF], U32, "wa_c0"))
+        wa_c, wa_s = quantize_wa(0, wa_g0, at(0, [P, HALF], U32, "wa_c0"))
         a0 = [bank(PACK + u, [P, 2, HALF], "a_pair%d" % u) for u in range(2)]
         for u, pair in enumerate(PAIRS):
             for v, t in enumerate(pair):
                 project(a0[u][:, v, :], xa_w, xa_s, t, wa_c[:], wa_s[:])
         wa_g1 = cast_wa(1)
 
-        bq0 = [slot("bq00", [P, 2, HALF], F32, "bq00"), at(14, [P, 2, HALF], F32, "bq01")]
+        bq0 = [slot("bq00", [P, 2, HALF], F32, "bq00"), at(20, [P, 2, HALF], F32, "bq01")]
         nc.vector.tensor_copy(bq0[1][:, 0, :], picked_b(0, 1))
         for t in (0, 2, 3):
             gather_on_scalar(bq0[t % 2][:, t // 2, :], 0, t)
@@ -229,10 +230,10 @@ def tile_picked_tokmax_none_po_kernel(
         for u in range(2):
             for t in range(PACK):
                 project(a1[u][:, t, :], xa_w, xa_s, t, wa_c[:, chunk(u)], wa_s[:, chunk(u)])
-        bq1 = at(16, [P, PACK, HALF], F32, "bq1")
+        bq1 = at(13, [P, PACK, HALF], F32, "bq1")
         for t in range(PACK):
             gather_on_scalar(bq1[:, t, :], 1, t)
-        w1s_d = at(14, [P, N], U8, "w1s_d")
+        w1s_d = at(20, [P, N], U8, "w1s_d")
         nc.vector.tensor_copy(
             out=w1s_d[:].rearrange("p (t m) -> p t m", t=PACK), in_=w1s[:].rearrange("p (m t) -> p t m", t=PACK)
         )

from contextlib import ExitStack

import concourse.mybir as mybir

K, T, S, N, H = 512, 2048, 512, 512, 512
FLOPS = 2 * S * K * H * 2 + 2 * S * N * H

F32 = mybir.dt.float32
BF16 = mybir.dt.bfloat16
I32 = mybir.dt.int32
U32 = mybir.dt.uint32
U16 = mybir.dt.uint16
U8 = mybir.dt.uint8
FP8X4 = mybir.dt.float8_e4m3fn_x4
FP4X4 = mybir.dt.float4_e2m1fn_x4
ACT = mybir.ActivationFunctionType
ALU = mybir.AluOpType

P = 128
PACK = 4
HALF = H // 2
CHUNK = 128
LINE = 4
KIB = 1024
WB_ON_SCALAR = (256, 112)
PAIRS = ((0, 2), (1, 3))


def tile_picked_tokmax_none_po_kernel(
    tc, x_words, x_scales, wa, wb, gt, w1_words, w1_scales, offs, two, fl, out_0, out_1, out_2
):
    nc = tc.nc
    with ExitStack() as ctx:
        keep = ctx.enter_context(tc.tile_pool(name="keep", bufs=1))
        placed = ctx.enter_context(tc.tile_pool(name="placed", bufs=1))
        psum = ctx.enter_context(tc.psum_pool(name="psum", bufs=1))

        def sb(shape, dtype, name):
            return keep.tile(shape, dtype, name=name, align_bytes=64)

        def slot(tag, shape, dtype, name):
            return keep.tile(shape, dtype, name=name, tag=tag, align_bytes=64)

        def at(kib, shape, dtype, name):
            return placed.tile(shape, dtype, name=name, offset=kib * KIB, align_bytes=64)

        def bank(i, shape, name):
            return psum.tile(shape, F32, name=name, tag="bank%d" % i)

        offs_t = keep.tile([P, S // 16], U16, name="offs_t")
        two_t = keep.tile([P, S // 16], U16, name="two_t")
        fl_t = keep.tile([P, H // 16], U16, name="fl_t")
        xw = sb([P, T], I32, "xw")
        xs = sb([P, T], U8, "xs")
        w1w = sb([P, 2 * N], U8, "w1w")
        w1s = sb([P, N], U8, "w1s")
        g = sb([P, PACK], F32, "g")

        wb_raw = [at(4 * h, [P, PACK, HALF], F32, "wb_raw%d" % h) for h in range(2)]
        wa_raw = [at(21, [P, PACK, HALF], F32, "wa_raw0"), sb([P, PACK, HALF], F32, "wa_raw1")]

        nc.vector.memset(xs[:].bitcast(I32), 0)
        nc.vector.memset(w1s[:].bitcast(I32), 0)

        wb_v = wb.rearrange("(p j) c -> p j c", j=PACK)
        wa_v = wa.rearrange("(p j) c -> p j c", j=PACK)

        def load_scale_rows(dst, src, queues):
            for q in range(4):
                queues[q].dma_start(out=dst[32 * q : 32 * q + 4, :].bitcast(I32), in_=src[0, 4 * q : 4 * q + 4, :].bitcast(I32))

        nc.sync.dma_start(out=w1w[:].bitcast(I32), in_=w1_words[0].bitcast(I32))
        nc.sync.dma_start(two_t[:], two)
        nc.sync.dma_start(offs_t[:], offs)
        load_scale_rows(xs, x_scales, (nc.sync, nc.sync, nc.scalar, nc.scalar))
        nc.sync.dma_start(out=wb_raw[0][:], in_=wb_v[:, :, 0:HALF])
        nc.sync.dma_start(out=xw[:], in_=x_words[0].rearrange("p n t -> p (n t)").bitcast(I32))
        nc.sync.dma_start(out=wb_raw[1][:], in_=wb_v[:, :, HALF:H])
        nc.sync.dma_start(out=wa_raw[0][:], in_=wa_v[:, :, 0:HALF])
        nc.sync.dma_start(fl_t[:], fl)
        nc.sync.dma_start(out=wa_raw[1][:], in_=wa_v[:, :, HALF:H])
        nc.sync.dma_start(out=g[:], in_=gt.rearrange("(p t) o -> p (t o)", t=PACK))
        load_scale_rows(w1s, w1_scales, (nc.sync,) * 4)

        def walk(ap):
            return ap.rearrange("p t (c i) -> p c t i", i=LINE)

        def woven(ap):
            return ap.rearrange("p (c i t) -> p c t i", i=LINE, t=PACK)

        def cast(copy, planes, grouped):
            copy(out=woven(grouped), in_=walk(planes))

        def quantize(codes, scales, values):
            nc.vector.quantize_mx(out=codes.bitcast(FP8X4), scales=scales, in_=values)

        def pick(table, lst, dealt):
            nc.vector.tensor_copy(dealt[:].rearrange("p (t m) -> p m t", t=PACK), table.indirect(lst[:]))
            return dealt

        def rows(t):
            return slice(t * P, (t + 1) * P)

        def half(h):
            return slice(h * HALF, (h + 1) * HALF)

        def chunk(c, per=1):
            return slice(c * CHUNK * per, (c + 1) * CHUNK * per)

        def project(acc, x_w, x_s, t, w_c, w_s):
            nc.tensor.matmul_mx(
                out=acc, lhsT=x_w[:, rows(t)].bitcast(FP8X4), lhsT_scale=x_s[:, rows(t)],
                rhs=w_c.bitcast(FP8X4), rhs_scale=w_s, start=True, stop=True,
            )

        w1w_d = sb([P, 2 * N], U8, "w1w_d")
        nc.vector.tensor_copy(
            out=w1w_d[:].rearrange("p (t m b) -> p t m b", t=PACK, b=2),
            in_=w1w[:].rearrange("p (m t b) -> p t m b", t=PACK, b=2),
        )
        xb_s = pick(xs[:], two_t, sb([P, S], U8, "xb_s"))
        xa_s = pick(xs[:], offs_t, sb([P, S], U8, "xa_s"))

        wb_g = [sb([P, HALF * PACK], BF16, "wb_g0"), at(11, [P, HALF * PACK], BF16, "wb_g1")]
        wb_c = at(19, [P, H], U32, "wb_c")
        wb_s = sb([P, H], U8, "wb_s")

        def quantize_wb(h):
            n = WB_ON_SCALAR[h]
            cast(nc.scalar.copy, wb_raw[h][:, :, 0:n], wb_g[h][:, 0 : n * PACK])
            if n < HALF:
                cast(nc.vector.tensor_copy, wb_raw[h][:, :, n:HALF], wb_g[h][:, n * PACK : HALF * PACK])
            quantize(wb_c[:, half(h)], wb_s[:, half(h)], wb_g[h][:])

        quantize_wb(0)
        xb_w = pick(xw[:].bitcast(U32), two_t, at(0, [P, S], U32, "xb_w"))
        quantize_wb(1)
        xa_w = pick(xw[:].bitcast(U32), offs_t, at(4, [P, S], U32, "xa_w"))

        b_acc = [[bank(PACK * (1 - h) + t, [P, HALF], "b_acc%d_%d" % (h, t)) for t in range(PACK)] for h in range(2)]
        for h in range(2):
            for t in range(PACK):
                project(b_acc[h][t][:], xb_w, xb_s, t, wb_c[:, half(h)], wb_s[:, half(h)])

        b_sb = [sb([P, H], F32, "b_sb%d" % t) for t in range(PACK)]

        def copy_b(copy, h, t):
            copy(out=b_sb[t][:, half(h)], in_=b_acc[h][t][:])

        def cast_wa(h):
            wa_g = at(12 - h, [P, HALF * PACK], BF16, "wa_g%d" % h)
            nc.gpsimd.tensor_scalar(
                out=wa_g[:].rearrange("p (c j) -> p c j", j=PACK), in0=wa_raw[h][:].rearrange("p j c -> p c j"),
                scalar1=1.0, scalar2=0.0, op0=ALU.mult, op1=ALU.add,
            )
            return wa_g

        def quantize_wa(h, wa_g, wa_c):
            wa_s = sb([P, HALF], U8, "wa_s%d" % h)
            quantize(wa_c[:], wa_s[:], wa_g[:])
            return wa_c, wa_s

        def picked_b(h, t):
            return b_sb[t][:].indirect(fl_t[:, h * HALF // 16 : (h + 1) * HALF // 16])

        def gather_on_scalar(out, h, t):
            nc.scalar.activation(out=out, in_=picked_b(h, t), func=ACT.Copy)

        def larger(out, acc, bq_ap):
            nc.vector.tensor_tensor(out=out, in0=acc[:], in1=bq_ap, op=ALU.max)

        def weigh(c, m):
            z = slot("z%d" % c, [P, CHUNK * PACK], BF16, "z%d" % c)
            nc.vector.tensor_tensor(
                out=woven(z[:]), in0=walk(m[:, :, chunk(c % 2)]),
                in1=g[:].unsqueeze(1).unsqueeze(3).to_broadcast([P, CHUNK // LINE, PACK, LINE]), op=ALU.mult,
            )
            return z

        def quantize_z(c, z, z_c):
            z_s = sb([P, CHUNK], U8, "z_s%d" % c)
            quantize(z_c[:], z_s[:], z[:])
            return z_c, z_s

        out_v = out_0.rearrange("(p t) j -> p t j", t=PACK)
        words_v = out_1[0].rearrange("p n r -> p (n r)").bitcast(I32)
        y_g = sb([P, H * PACK], BF16, "y_g")
        y_s = sb([P, H], U8, "y_s")

        def mix(c, z_q, emptied, y):
            z_c, z_s = z_q
            per = PACK // len(emptied)
            for u, (which, copy) in enumerate(emptied):
                acc = bank(which, [P, per, CHUNK], "y_acc%d" % which)
                for v in range(per):
                    t = u * per + v
                    nc.tensor.matmul_mx(
                        out=acc[:, v, :], lhsT=w1w_d[:, 2 * P * t : 2 * P * (t + 1)].bitcast(FP4X4), lhsT_scale=w1s_d[:, rows(t)],
                        rhs=z_c[:].bitcast(FP8X4), rhs_scale=z_s[:], start=True, stop=True,
                    )
                copy(out=y[:, u * per : (u + 1) * per, :], in_=acc[:])

        def round_y(copy, c, y):
            cast(copy, y, y_g[:, chunk(c, PACK)])

        on_scalar, on_vector = nc.scalar.copy, nc.vector.tensor_copy

        wa_g0 = cast_wa(0)
        for t in range(PACK):
            copy_b(on_scalar, 0, t)
        for t in range(PACK):
            copy_b(on_vector if t % 2 else on_scalar, 1, t)
        wa_c, wa_s = quantize_wa(0, wa_g0, at(0, [P, HALF], U32, "wa_c0"))
        a0 = [bank(PACK + u, [P, 2, HALF], "a_pair%d" % u) for u in range(2)]
        for u, pair in enumerate(PAIRS):
            for v, t in enumerate(pair):
                project(a0[u][:, v, :], xa_w, xa_s, t, wa_c[:], wa_s[:])
        wa_g1 = cast_wa(1)

        bq0 = [slot("bq00", [P, 2, HALF], F32, "bq00"), at(20, [P, 2, HALF], F32, "bq01")]
        nc.vector.tensor_copy(bq0[1][:, 0, :], picked_b(0, 1))
        for t in (0, 2, 3):
            gather_on_scalar(bq0[t % 2][:, t // 2, :], 0, t)
        m0 = slot("m", [P, PACK, HALF], F32, "m0")
        for u in range(2):
            larger(m0[:, u:PACK:2, :], a0[u], bq0[u][:])

        wa_c, wa_s = quantize_wa(1, wa_g1, slot("bq00", [P, HALF], U32, "wa_c1"))
        a1 = [bank(PACK + 2 + u, [P, PACK, CHUNK], "a_chunk%d" % u) for u in range(2)]
        for u in range(2):
            for t in range(PACK):
                project(a1[u][:, t, :], xa_w, xa_s, t, wa_c[:, chunk(u)], wa_s[:, chunk(u)])
        bq1 = at(13, [P, PACK, HALF], F32, "bq1")
        for t in range(PACK):
            gather_on_scalar(bq1[:, t, :], 1, t)
        w1s_d = at(20, [P, N], U8, "w1s_d")
        nc.vector.tensor_copy(
            out=w1s_d[:].rearrange("p (t m) -> p t m", t=PACK), in_=w1s[:].rearrange("p (m t) -> p t m", t=PACK)
        )
        z0 = weigh(0, m0)
        z1 = weigh(1, m0)
        y01 = sb([P, PACK, HALF], F32, "y01")
        for c, z in enumerate((z0, z1)):
            mix(c, quantize_z(c, z, sb([P, CHUNK], U32, "z_c%d" % c)), [(c, on_scalar)], y01[:, :, chunk(c)])
        nc.sync.dma_start(out=out_v[:, :, half(0)], in_=y01[:])
        for c in range(2):
            round_y(on_scalar, c, y01[:, :, chunk(c)])

        m1 = slot("m", [P, PACK, HALF], F32, "m1")
        for u in range(2):
            larger(m1[:, :, chunk(u)], a1[u], bq1[:, :, chunk(u)])
        z2 = weigh(2, m1)
        z3 = weigh(3, m1)
        z_q2 = quantize_z(2, z2, sb([P, CHUNK], U32, "z_c2"))
        z_q3 = quantize_z(3, z3, sb([P, CHUNK], U32, "z_c3"))
        y2 = sb([P, PACK, CHUNK], F32, "y2")
        y3 = sb([P, PACK, CHUNK], F32, "y3")
        mix(2, z_q2, [(2, on_scalar), (3, on_vector)], y2[:])
        for u in range(2):
            nc.sync.dma_start(out=out_v[:, 2 * u : 2 * u + 2, chunk(2)], in_=y2[:, 2 * u : 2 * u + 2, :])
        mix(3, z_q3, [(4, on_scalar), (5, on_scalar)], y3[:])
        nc.sync.dma_start(out=out_v[:, :, chunk(3)], in_=y3[:])

        y_c = slot("z3", [P, H], I32, "y_c")
        quantize(y_c[:, half(0)], y_s[:, half(0)], y_g[:, 0 : HALF * PACK])
        round_y(on_vector, 2, y2[:])
        round_y(on_vector, 3, y3[:])
        for c in (2, 3):
            quantize(y_c[:, chunk(c)], y_s[:, chunk(c)], y_g[:, chunk(c, PACK)])
        nc.sync.dma_start(out=words_v, in_=y_c[:])
        for q in range(4):
            eng = nc.scalar if q % 2 else nc.sync
            eng.dma_start(out=out_2[0, 4 * q : 4 * q + 4, :].bitcast(I32), in_=y_s[32 * q : 32 * q + 4, :].bitcast(I32))
